import numpy as np, ml_dtypes
CORES = [16,17,18,19,32,33,34,35]
N = 8
import mx_ref
BF = ml_dtypes.bfloat16
def gentries(a):
    return np.ascontiguousarray(a.reshape(8, 16, -1).transpose(0, 2, 1)).reshape(8, -1)
def gtable(e):
    e = np.asarray(e); return np.ascontiguousarray(e.reshape(8, -1, 16).transpose(0, 2, 1)).reshape(128, -1).astype(np.int32)
def gcols(t, e):
    v = np.concatenate([t.reshape(8, 16, -1, 4), np.zeros((8, 16, 1, 4), BF)], axis=2)
    return np.ascontiguousarray(np.stack([v[g][:, e[g]] for g in range(8)])).reshape(128, -1)
def tile(rs):
    return np.stack(rs, axis=2).reshape(128, -1).astype(BF)
def pick(q, e):
    c = np.concatenate([q[0].reshape(128, -1, 4), np.zeros((128, 1, 4), np.uint8)], axis=1); s = np.concatenate([q[1], np.ones((16, 1), np.uint8)], axis=1)
    return (np.ascontiguousarray(c[:, e].reshape(128, -1)), np.ascontiguousarray(s[:, e]))
def join(*qs):
    return (np.concatenate([q[0] for q in qs], axis=1), np.concatenate([q[1] for q in qs], axis=1))
def put(q, e, v):
    c, s = q[0].reshape(128, -1, 4).copy(), q[1].copy(); c[:, e] = v[0].reshape(128, -1, 4); s[:, e] = v[1]
    return (c.reshape(128, -1), s)
def pk(c, s):
    return (np.ascontiguousarray(c), mx_ref.live(s))
def emit(q):
    return q[0], q[1]
def packed(v, rng):
    q = [mx_ref.quantize(np.ascontiguousarray(v[r])) for r in range(N)]
    return np.stack([a for a, b in q]), np.stack([mx_ref.plane(b, rng) for a, b in q])
def values_of_codes():
    e, c = np.zeros((128, 128, 4), np.float32), np.zeros((128, 2, 4), np.uint8)
    e[np.arange(128), np.arange(128), 0] = 1
    c[:127, :, 0] = np.arange(256).reshape(2, 128).T[:127]
    return mx_ref.matmul(mx_ref.quantize(e.reshape(128, 512).astype(BF)), (c.reshape(128, 8), np.full((16, 2), 127, np.uint8))).T.reshape(-1).astype(np.float64)
CODE_VALUE, SCALE_VALUE = values_of_codes(), 2.0 ** (np.arange(256) - 127.0)
def decode(q):
    return (CODE_VALUE[q[0]].reshape(16, 8, -1, 4) * SCALE_VALUE[q[1]][:, None, :, None] + 0.0).reshape(128, -1).astype(np.float32)
def f(rng, *shape):
    return mx_ref.flush((rng.standard_normal(shape, dtype=np.float32) * np.exp2(rng.integers(-2, 3, shape[:-1] + (1,)))).astype(BF))
def wide(rng, *shape, cols=0):
    v = rng.standard_normal(shape, dtype=np.float32) * np.exp2(rng.integers(-12, 13, shape)).astype(np.float32)
    if cols: v *= np.repeat(np.exp2(rng.integers(-cols, cols + 1, shape[:-2] + (1, shape[-1] // 4))) * (rng.random(shape[:-2] + (1, shape[-1] // 4)) > 0.0625), 4, axis=-1).astype(np.float32)
    return mx_ref.flush(v.astype(BF))
C, K, R = 384, 192, 3
def numbers_of(rng):
    return np.array(f(rng, N, 128, 4 * C)), np.array(f(rng, N, 128, 512)), np.array(f(rng, N, 128, 512))
def operands(rng):
    return rng.integers(0, C, (N, 8, C))
def layers(rng, still=[]):
    w = np.array(f(rng, N, 128, 2048)).reshape(N, 8, 16, 4, 8, 16, 4)
    for i in still:
        w[:, :, i] = 0
        w[:, :, :, :, :, i] = 0
    return w
def clear(u):
    a = u.reshape(N, 128, 128, 4)
    for i in range(5): a[:, :, i::16] = 0
    return a
def given(rng, x, l, m, u, v, w):
    c, s = packed(np.ascontiguousarray(w).reshape(N, 128, 2048), rng)
    return {"x": x.reshape(N, 128, 4 * C).astype(BF), "l": np.stack([gtable(l[r]) for r in range(N)]), "m": np.stack([gtable(m[r]) for r in range(N)]), "u": u.reshape(N, 128, 512), "v": v, "wc": c, "ws": s}
def setup_inputs(rng):
    x, u, v = numbers_of(rng)
    return given(rng, x, operands(rng), operands(rng), u, v, layers(rng))
def setup_inputs_ties(rng):
    x, u, v = numbers_of(rng)
    x = x.reshape(N, 8, 16, C, 4)
    x[:, :, 0] = 0
    x[:, :, 0, :, 0] = np.exp2(rng.integers(0, 3, (N, 8, C))).astype(BF)
    x[:, :, 1] = rng.integers(-1, 2, (N, 8, C, 4)).astype(np.float32).astype(BF)
    a = clear(u)
    o = rng.permutation(N)
    for r in range(N):
        for h in range(0, 128, 16):
            a[r, h, h, 0] = 0.0 if r == o[0] else -1.0 if r == o[1] else 1.0
            for b in range(4): a[r, h + 1, h + 1 + b, b] = 1.0
    e = o[2]
    x[e, :, 8:] = 0
    x[e, :, 8, :, 0] = 1.96875
    for i in range(6):
        x[e, :, 9 + i, :, 0] = ((1 + 0.125 * rng.integers(0, 8, (8, C))) * 2.0 ** -(10 + i)).astype(np.float32).astype(BF)
        for h in range(0, 128, 16):
            a[e, h, h, 0] = 0.0
            a[e, h + 9 + i, h, 0] = 2.0 ** (10 + i)
    return given(rng, x, operands(rng), operands(rng), a, v, layers(rng, [0, 1, 8, 9, 10, 11, 12, 13, 14, 15]))
def setup_inputs_near(rng):
    x, u, v = numbers_of(rng)
    x = x.astype(np.float32).reshape(N, 8, 16, C, 4)
    x[:, :, 0] = 0
    x[:, :, 8:] = 0
    a = clear(u)
    o = rng.permutation(N) % 4
    for r in range(N):
        if o[r] < 3:
            s = rng.integers(0, 16, (8, C))
            x[r, :, 8] = ((s[:, :, None] >> np.arange(4)) & 1) * np.exp2(np.arange(4) - 23.0)
            x[r, :, 12] = rng.integers(-1, 2, (8, C, 4)) * 2.0 ** -16
        else:
            x[r, :, 10] = rng.integers(-1, 2, (8, C, 4)) * 2.0 ** -29
            x[r, :, 12, :, :2] = (rng.integers(0, 2, (8, C, 2)) * 2.0 - 1.0) * 2.0 ** -30
            x[r, :, 12, :, 2:] = rng.integers(-1, 2, (8, C, 2)) * 2.0 ** -29
        if o[r] < 2:
            x[r, :, 0, :, 0] = rng.integers(0, 2, (8, C)) * 2.0 - 1.0 if o[r] == 0 else -1.0
            x[r, :, 11, :, 0] = 2.0 ** -10
        for g in rng.permutation(8)[:4]:
            c = rng.integers(C)
            x[r, g, 8:, c] = 0
            x[r, g, 0, c, 0] = 2.0 ** 29 * rng.choice([-1.0, 1.0])
            x[r, g, 12, c] = 2.0 ** 29 * rng.choice([-1.0, 1.0], 4)
        k = 1.0 if o[r] == 0 else 2.0 ** -30
        for h in range(0, 128, 16):
            a[r, h, h, 0] = k
            if o[r] < 3:
                a[r, h + 8, h] = k
                a[r, h + 11, h, 0] = k
            else: a[r, h + 10, h] = (np.array([1.0, 1.125, 1.25, 1.5]) * k).astype(BF)
            for b in range(4): a[r, h + 12, h + 1 + b, b] = k
    return given(rng, x, operands(rng), operands(rng), a, v, layers(rng, [0, 8, 9, 10, 11, 12, 13, 14, 15]))
def setup_inputs_late(rng):
    x, u, v = numbers_of(rng)
    x = x.reshape(N, 8, 16, C, 4)
    x[:, :, 0] = (rng.permutation(N) % 2 * 2.0 - 1.0).astype(BF)[:, None, None, None]
    a = clear(u)
    for h in range(0, 128, 16):
        a[:, h, h] = 1.0
        for b in range(4): a[:, h, h + 1 + b, b] = 1.0
    return given(rng, x, operands(rng), operands(rng), a, v, layers(rng))
def setup_inputs_huge(rng):
    x, u, v = numbers_of(rng)
    o = rng.permutation(N)
    c = np.where(np.argsort(rng.random((N, C)), axis=1) < C // 4, 1.0, -1.0)[:, None, None, :, None] * 2.0 ** 30
    x = (0.6 + 0.09 * rng.random((N, 8, 16, C, 4))) * c
    x[o == 0] = (0.9375 + 0.0625 * rng.integers(0, 2, (1, 8, 16, C, 4))) * c[o == 0]
    a = 2.0 ** 30 * (1.0 - 0.1 * rng.random((N, 128, 8, 4)))
    a[o == 0] = 2.0 ** 30
    for r in range(N): a[r] *= (rng.permutation(8) % 2 * 2.0 - 1.0)[None, :, None]
    u = u.reshape(N, 128, 128, 4)
    u[:, :, ::16] = a.astype(np.float32).astype(BF)
    w = np.zeros((N, 128, 4, 128, 4), np.float32)
    i = np.arange(128)
    for b in range(4): w[:, i, b, i, b] = -2
    return given(rng, x.astype(np.float32), operands(rng), operands(rng), u, v, w.astype(BF))
def setup_inputs_spread(rng):
    x, u, v = numbers_of(rng)
    x = np.array(wide(rng, N, 128, 4 * C, cols=6)).reshape(N, 16, 8, C, 4)
    t = np.exp2(-rng.integers(8, 15, (N, 16, 8, C // 8, 4)).astype(np.float64)) * (1 + (2 * rng.integers(0, 64, (N, 16, 8, C // 8, 4)) + 1) * 2.0 ** -7)
    t[:, :, 0, :, 0] = 1.96875
    x[:, :, :, 3::8] = (t * rng.choice([-1.0, 1.0], t.shape)).astype(np.float32).astype(BF)
    l, m = 2 * rng.integers(0, C // 2, (N, 8, C)), 2 * rng.integers(0, C // 2, (N, 8, C))
    e = rng.permutation(N)
    l[e[0]], m[e[0]] = C - 1, 0
    l[e[1]] = m[e[1]]
    l[e[2]], m[e[2]] = np.arange(C), C - 1 - np.arange(C)
    l[e[3]], m[e[3]] = rng.integers(0, 2, (8, C)), rng.integers(0, 2, (8, C))
    return given(rng, x, l, m, u, v, layers(rng))
def check_inputs(d):
    b = []
    for k in ("x", "u", "v"):
        a = np.abs(d[k].astype(np.float32))
        if not (np.isfinite(a).all() and ((a == 0) | (a >= 2.0 ** -30) & (a <= 2.0 ** 30)).all()): b.append("a value of " + k)
    for k in ("l", "m"):
        if not ((d[k] >= 0) & (d[k] < C)).all(): b.append("an entry of " + k)
    none, least, most = [emit(mx_ref.quantize(np.full((128, 16), k, np.float32).astype(BF)))[1][0, 0] for k in (0.0, 2.0 ** -30, 2.0 ** 30)]
    for r in range(N):
        if ((d["wc"][r] == 0x7F) | (d["wc"][r] == 0xFF)).any(): b.append("wc: a code that is no number")
        s = mx_ref.live(d["ws"][r])
        if ((s != none) & ((s < least) | (s > most))).any(): b.append("ws: a scale out of range")
    return b
def reference(x, l, m, u, v, wc, ws):
    qu = [mx_ref.quantize(u[r]) for r in range(N)]
    lay = [pk(wc[r], ws[r]) for r in range(N)]
    first, second = [gentries(l[r]) for r in range(N)], [gentries(m[r]) for r in range(N)]
    now = [x[r] for r in range(N)]
    lanes = np.arange(8)[:, None]
    left, right = np.zeros((N, 8, K), np.int64), np.zeros((N, 8, K), np.int64)
    for t in range(R):
        own, packs = [], []
        for r in range(N):
            q = mx_ref.quantize(now[r])
            own.append(decode(q).astype(BF))
            s = mx_ref.matmul(qu[r], q) + np.float32(0.0)
            n = np.argsort(-s[::16], axis=1, kind="stable")[:, :K]
            a, b = first[r][lanes, n], second[r][lanes, n]
            word = np.stack([s[i::16] > 0 for i in range(1, 5)])
            wa, wb = word[:, lanes, a], word[:, lanes, b]
            straight = np.count_nonzero(wa == wa[:, :1], axis=0) + np.count_nonzero(wb == wb[:, :1], axis=0)
            crossed = np.count_nonzero(wb == wa[:, :1], axis=0) + np.count_nonzero(wa == wb[:, :1], axis=0)
            left[r] = np.where(crossed > straight, b, a)
            right[r] = np.where(crossed > straight, a, b)
            z = (gcols(own[r], left[r]).astype(np.float32) - gcols(own[r], right[r]).astype(np.float32)) * np.float32(0.5)
            packs.append(mx_ref.quantize(z.astype(BF)))
        for r in range(N):
            e = (r + 1 + t) % N
            h = mx_ref.quantize(tile([mx_ref.matmul(pick(lay[e], np.arange(128 * b, 128 * b + 128)), packs[r]) * np.float32(0.03125) for b in range(4)]))
            who = np.full((8, C), -1)
            for k in reversed(range(K)): who[np.arange(8), left[r][:, k]] = k
            now[r] = (own[r].astype(np.float32) + gcols(decode(h).astype(BF), who).astype(np.float32)).astype(BF)
    y, ol = np.zeros((N, 128, C), np.float32), np.zeros((N, 8, 2 * K), np.float32)
    oc, osc = np.zeros((N, 128, 4 * C), np.uint8), np.zeros((N, 16, C), np.uint8)
    for r in range(N):
        q = mx_ref.quantize(now[r])
        y[r] = mx_ref.matmul(mx_ref.quantize(v[r]), q)
        ol[r] = np.concatenate([left[r], right[r]], axis=1)
        oc[r], osc[r] = emit(q)
    return {"y": y, "ol": ol, "oc": oc, "osc": osc}

@@ -1,0 +1,549 @@
+import numpy as np
+from concourse.mybir import dt, AluOpType, AxisListType, ActivationFunctionType
+
+A = AluOpType
+F = ActivationFunctionType
+C, K, R = 384, 192, 3
+BIG = 2.0 ** 80
+BF, F32, I32, U16, Q4, U8 = "bfloat16", "float32", "int32", "uint16", "float8_e4m3fn_x4", "uint8"
+WIDE = {BF: 2, F32: 4, I32: 4, U16: 2, Q4: 4, U8: 1}
+TILES = [384, 320, 256, 192, 128, 128]
+SLOTS = [[0, 23, 22, 21], [20, 19, 18, 17], [16, 15, 14, 13], [12, 11, 10, 9], [8, 7, 6, 5], [4, 3, 2, 1]]
+TOFF = [sum(TILES[:i]) for i in range(6)]
+S_ROWS = [(23, 22), (23, 22), (23, 22)]
+ROFF = [8 * c * (c - 1) for c in range(25)]
+SAMEQ = True
+CY, PE, GAT, SCA, WAKE = 1.0, 0.6, 1.5, 3.5, 80.0
+PASSES = 7000
+
+
+def _sb(n, d):
+    return ("sbuf", [128, n], d)
+
+
+SCRATCH = {
+    "xt": _sb(4 * C, BF), "qx": _sb(C, Q4), "sx": _sb(C, U8),
+    "ut": _sb(512, BF), "qu": _sb(128, Q4), "su": _sb(128, U8), "qu2": _sb(256, Q4), "su2": _sb(256, U8),
+    "vt": _sb(512, BF), "qv": _sb(128, Q4), "sv": _sb(128, U8),
+    "wq": _sb(512, Q4), "wp": _sb(512, U8),
+    "wq0": _sb(512, Q4), "wp0": _sb(512, U8), "wq1": _sb(512, Q4), "wp1": _sb(512, U8), "wq2": _sb(512, Q4), "wp2": _sb(512, U8),
+    "l32": _sb(24, I32), "m32": _sb(24, I32), "lu": _sb(24, U16), "mu": _sb(24, U16),
+    "half": _sb(516, BF), "et": _sb(516, BF), "qe": _sb(512, Q4), "se": _sb(512, U8),
+    "grp": _sb(512, BF), "one01": _sb(512, BF), "ktmp": _sb(512, BF), "kt": _sb(2048, BF), "qk": _sb(512, Q4), "sk": _sb(512, U8),
+    "ct": _sb(4 * 1408, BF), "qc": _sb(1408, Q4), "sc": _sb(1408, U8),
+    "jk": _sb(4416, BF), "sg": _sb(4416, BF),
+    "cin": _sb(3 * 128, F32), "sm": _sb(5 * 128, F32),
+    "p32": _sb(24, I32), "pu": _sb(24, U16), "c32": _sb(12, I32), "repu": _sb(12, U16),
+    "pi": _sb(8, I32), "col": _sb(16, F32), "pk32": _sb(16, I32), "pkf": _sb(8, F32), "pku": _sb(16, U16),
+    "cmin": _sb(C, F32), "khold": _sb(C, F32), "cxr": _sb(C, F32), "cxw": _sb(C, F32), "camp": _sb(K, F32), "keep": _sb(C, BF),
+    "rw": _sb(32, F32), "base": _sb(24, F32), "base2": _sb(24, F32), "m48": _sb(48, F32),
+    "iot": _sb(C, F32), "lmb": _sb(C, F32), "lm": _sb(C, F32), "wh": _sb(3 * 400, F32),
+    "m1": _sb(C, F32), "hh": _sb(C, F32), "rd": _sb(C, BF), "rs": _sb(24, F32), "xs": _sb(C, F32), "rk": _sb(24, U16),
+    "sgb": _sb(C, BF), "bw": _sb(C, BF), "x1": _sb(C, F32), "pay": _sb(C, BF), "pw": _sb(416, BF),
+    "yt": _sb(544, BF), "qy": _sb(136, Q4), "sy": _sb(136, U8),
+    "w48": _sb(48, F32), "ab": _sb(24, F32), "ab2": _sb(24, F32), "ee": _sb(12, F32), "bs": _sb(12, F32),
+    "ppi": _sb(12, I32), "fl": _sb(12, I32), "fe": _sb(12, F32), "lr": _sb(24, F32), "lru": _sb(24, U16),
+    "tv": _sb(4 * 576, BF), "ln": _sb(4 * K, BF), "mt": _sb(4 * K, BF), "qm": _sb(K, Q4), "smm": _sb(K, U8),
+    "ht": _sb(4 * K, BF), "qh": _sb(K, Q4), "sh": _sb(K, U8),
+    "ff": _sb(K, F32), "eq": _sb(K, F32), "es": _sb(K, F32), "d1": _sb(12, F32), "d2": _sb(12, F32), "du": _sb(24, U16),
+    "xw": _sb(C, F32), "wu": _sb(24, U16), "olu": _sb(24, U16), "olf": _sb(C, F32), "yf": _sb(C, F32),
+    "ps": ("psum", [128, 4096], F32),
+}
+NDMA = 24
+SEMAPHORES = ["cv", "cs", "cp", "cg", "arr0", "arr1", "arr2", "sent"] + ["d%d" % i for i in range(NDMA)]
+CSEM = {"v": "cv", "s": "cs", "p": "cp", "g": "cg"}
+
+
+def v(name, a=0, b=None, s=1):
+    if b is None:
+        b = SCRATCH[name][1][1]
+    return (name, a, b, s)
+
+
+def bank(i, n, a=0, s=1):
+    return ("ps", 512 * i + a, 512 * i + n, s)
+
+
+def ind(win, off):
+    return ("ind", win, off)
+
+
+def _mask(w):
+    if w[0] == "ps":
+        return 1 << (w[1] // 512)
+    m = 0
+    if w[3] == 1:
+        return ((1 << (w[2] - w[1])) - 1) << w[1]
+    for i in range(w[1], w[2], w[3]):
+        m |= 1 << i
+    return m
+
+
+def _n(w):
+    return 16 * _n(w[2]) if w[0] == "ind" else len(range(w[1], w[2], w[3]))
+
+
+def _vcost(o, i, base=None):
+    if o[0] == "ind":
+        return 50 + _n(i) * SCA * CY
+    if i[0] == "ind":
+        return 50 + _n(i) * max(GAT, base or 0) * CY
+    if base is None:
+        base = 0.5 if WIDE[SCRATCH[o[0]][2]] == 2 and WIDE[SCRATCH[i[0]][2]] == 2 else 1.0
+    return max(64, _n(i) * base) * CY
+
+
+def build(T, topo, core):
+    ops = []
+
+    def ap(w, cast=None):
+        if not isinstance(w, tuple):
+            return w
+        if w[0] == "ind":
+            return ap(w[1], cast).indirect(ap(w[2]))
+        r = T[w[0]][:, w[1]:w[2]:w[3]] if w[3] != 1 else T[w[0]][:, w[1]:w[2]]
+        return r.bitcast(cast) if cast is not None else r
+
+    def flat(ws):
+        r = []
+        for w in ws:
+            if isinstance(w, tuple):
+                r += [w[1], w[2]] if w[0] == "ind" else [w]
+        return r
+
+    def add(q, fn, rd, wr, ns, kind="c"):
+        rd, wr2 = flat(rd), []
+        for w in wr:
+            if w[0] == "ind":
+                wr2.append(w[1])
+                rd.append(w[2])
+            else:
+                wr2.append(w)
+        ops.append((q, fn, rd, wr2, kind, ns))
+
+    def ts(o, i, s1, op0, s2=None, op1=None):
+        if op1 is None:
+            add("v", lambda e: e.tensor_scalar(ap(o), ap(i), ap(s1), None, op0), [i, s1], [o], _vcost(o, i))
+        else:
+            add("v", lambda e: e.tensor_scalar(ap(o), ap(i), ap(s1), ap(s2), op0, op1), [i, s1, s2], [o], _vcost(o, i))
+
+    def tt(o, a, b, op):
+        add("v", lambda e: e.tensor_tensor(ap(o), ap(a), ap(b), op), [a, b], [o], _vcost(o, a, 1.0 if "ps" in (a[0], b[0]) else 2.0))
+
+    def cp(o, i, cast=None):
+        add("v", lambda e: e.tensor_copy(ap(o, cast), ap(i, cast)), [i], [o], _vcost(o, i))
+
+    def ms(o, c):
+        add("v", lambda e: e.memset(ap(o), c), [], [o], _vcost(o, o))
+
+    def scan(o, a, b, init, op0, op1):
+        add("v", lambda e: e.tensor_tensor_scan(ap(o), ap(a), ap(b), init, op0, op1), [a, b], [o], _vcost(o, a))
+
+    def turn(o, i):
+        add("v", lambda e: e.transpose(ap(o), ap(i)), [i], [o], _vcost(o, i))
+
+    def quant(q, s, i):
+        add("v", lambda e: e.quantize_mx(ap(q), ap(s), ap(i)), [i], [q, s], 12 + 0.265 * CY * _n(i))
+
+    def act(o, i, f, bias=None, scale=None, acc=None):
+        def fn(e):
+            kw = {}
+            if bias is not None:
+                kw["bias"] = ap(bias)
+            if scale is not None:
+                kw["scale"] = ap(scale)
+            if acc is not None:
+                kw["accum_out"] = ap(acc)
+            return e.activation(ap(o), ap(i), f, **kw)
+        add("s", fn, [i, bias, scale], [o] + ([acc] if acc is not None else []),
+            60 + (20 if acc is not None else 0) + _n(i) * CY * (GAT if i[0] == "ind" else 1))
+
+    def mm(o, wq, ws, xq, xs, start=True, stop=True):
+        add("p", lambda e: e.matmul_mx(ap(o), ap(wq), ap(ws), ap(xq), ap(xs), start, stop), [wq, ws, xq, xs], [o], (_n(xq) + 16) * PE)
+
+    def iota(o, pat, base, cm):
+        if SCRATCH[o[0]][2] == I32:
+            add("g", lambda e: e.iota(ap(o), pat, base, cm), [], [o], 130 + 2 * CY * _n(o))
+        else:
+            add("g", lambda e: e.iota(ap(o), pat, base, cm, allow_small_or_imprecise_dtypes=True), [], [o], 130 + 2 * CY * _n(o))
+
+    def sel(o, i, pat, op, fill, base, cm):
+        add("g", lambda e: e.affine_select(ap(o), ap(i), pat, op, fill, base, cm), [i], [o], 170 + 2 * CY * _n(o))
+
+    def dma(q, o, i, rd, wr, ns=2500):
+        add(q, lambda e: e.dma_start(o(), i()), rd, wr, ns, "d")
+
+    rank = T.rank_of(core)
+    n = len(T.cores)
+
+    def send(t):
+        dst = T.cores[(rank - 1 - t) % n]
+        rid, pid = topo.addr(dst)[0], topo.addr(dst)[1]
+        m = topo.mask(core, dst)
+        cnt = len(topo.engines(core, dst))
+        add("g", lambda e: e.remote_dma(ap(v("wq%d" % t), dt.uint8), ap(v("wq"), dt.uint8), T.sem["arr%d" % t], T.sem.sent, pid, rid, m),
+            [v("wq")], [v("wq%d" % t, 0, 1)], 9000, ("r", cnt))
+        add("g", lambda e: e.remote_dma(ap(v("wp%d" % t)), ap(v("wp")), T.sem["arr%d" % t], T.sem.sent, pid, rid, m),
+            [v("wp")], [v("wp%d" % t, 0, 1)], 9000, ("r", cnt))
+
+    def arrived(t):
+        src = T.cores[(rank + 1 + t) % n]
+        cnt = 2 * len(topo.engines(src, core))
+        add("p", lambda e: e.wait_ge(T.sem["arr%d" % t], cnt), [v("qm")], [v("wq%d" % t), v("wp%d" % t)], 1, "w")
+
+    def c1(name, j):
+        return v(name, j, j + 1)
+
+    dma("y", lambda: T.ut[:], lambda: T.u[:], [], [v("ut")])
+    dma("s", lambda: T.xt[:, 768:1536], lambda: T.x[:, 768:1536], [], [v("xt", 768, 1536)], 3000)
+    dma("y", lambda: T.xt[:, 0:768], lambda: T.x[:, 0:768], [], [v("xt", 0, 768)], 3000)
+    dma("y", lambda: T.l32[:], lambda: T.l[:], [], [v("l32")])
+    dma("y", lambda: T.m32[:], lambda: T.m[:], [], [v("m32")])
+    dma("y", lambda: T.wq[:].bitcast(dt.uint8), lambda: T.wc[:], [], [v("wq")], 4000)
+    dma("y", lambda: T.wp[:], lambda: T.ws[:], [], [v("wp")], 4000)
+    dma("y", lambda: T.vt[:], lambda: T.v[:], [], [v("vt")])
+
+    ms(v("cin", 0, 128), BIG)
+    ms(v("cin", 128, 256), 1024.0)
+    ms(v("cin", 256, 384), 64.0)
+    ms(v("half"), -0.5)
+    iota(v("p32"), [[0, 24]], 0, 1)
+    sel(v("sm", 0, 128), v("cin", 0, 128), [[1, 128]], A.is_equal, -BIG, 0, -1)
+    sel(v("sm", 128, 256), v("cin", 0, 128), [[1, 128]], A.is_gt, -BIG, 0, -1)
+    iota(v("pk32"), [[0, 2], [16, 8]], 0, 0)
+    iota(v("iot"), [[1, C]], 0, 0)
+    iota(v("grp"), [[1, 8], [0, 64]], 0, 0)
+    iota(v("keep"), [[0, 24], [64, 16]], 0, 0)
+    send(0)
+    sel(v("sm", 256, 384), v("cin", 128, 256), [[1, 128]], A.is_equal, 0.0, 0, -1)
+    sel(v("sm", 384, 512), v("sm", 256, 384), [[1, 128]], A.is_ge, -4096.0, 0, -1)
+    iota(v("base"), [[16, 24]], 15, 0)
+    sel(v("et"), v("half"), [[-1, 516]], A.is_equal, 0.0, 3, 4)
+    iota(v("one01"), [[0, 128], [-1, 2], [0, 2]], 1, 0)
+    sel(v("kt", 512, 1024), v("one01"), [[0, 8], [-1, 16], [0, 4]], A.is_equal, 0.0, 0, 1)
+    sel(v("ktmp"), v("one01"), [[-1, 128], [0, 4]], A.is_equal, 0.0, 0, 1)
+    iota(v("m48"), [[0, 12], [1, 2], [0, 2]], 0, 0)
+    sel(v("sm", 512, 640), v("cin", 256, 384), [[1, 128]], A.is_equal, 1.0, 1, -1)
+    iota(v("c32"), [[1, 12]], 0, 0)
+    iota(v("wh", 0, 400), [[1, 400]], K, 0)
+    send(1)
+    send(2)
+    iota(v("wh", 400, 1200), [[0, 2], [1, 400]], K, 0)
+
+    cp(v("pu"), v("p32"))
+    ts(c1("pi", 0), c1("p32", 0), 1, A.bitwise_and)
+    ts(c1("pi", 1), c1("p32", 0), 2, A.logical_shift_right, 2, A.bitwise_and)
+    ts(c1("pi", 2), c1("p32", 0), 15, A.bitwise_and)
+    ts(c1("pi", 3), c1("p32", 0), 4, A.logical_shift_right, 1, A.bitwise_and)
+    ts(c1("pi", 4), c1("p32", 0), 4, A.logical_shift_right)
+    cp(v("col", 0, 5), v("pi", 0, 5))
+    q_, h_, g_, wt_, r2_, r2b_, hq_, nh_, junk_ = [c1("col", j) for j in range(2, 11)]
+    cp(v("pku", 0, 8), v("pk32", 0, 8))
+    ts(v("pkf"), v("pk32", 8, 16), c1("col", 0), A.add, c1("col", 1), A.add)
+    ts(v("pku", 8, 16), v("pkf"), 1.0, A.add)
+    act(v("cmin"), ind(v("sm", 0, 128), v("pu")), F.Copy)
+    act(v("khold"), ind(v("sm", 128, 256), v("pu")), F.Copy)
+    for i in range(6):
+        ms(v("ct", 4 * (TOFF[i] + 16 * SLOTS[i][3]), 4 * (TOFF[i] + TILES[i])), 0.0)
+    ms(c1("rs", 0), 0.0)
+    ms(v("pw", 0, 16), 0.0)
+    ms(v("yt", 384, 544), 0.0)
+    ms(v("rw", 0, 16), 0.0)
+    ms(v("rw", 0, 14, 13), 1.0)
+    ms(v("rw", 1, 13, 11), 16.0)
+    ms(v("rw", 5, 9, 3), 256.0)
+    ms(v("rw", 4, 10, 5), 4096.0)
+    quant(v("qu"), v("su"), v("ut"))
+    for j in range(2):
+        cp(v("qu2", 128 * j, 128 * j + 128), ind(v("qu"), v("pku", 8 * j, 8 * j + 8)), dt.uint32)
+        act(v("su2", 128 * j, 128 * j + 128), ind(v("su"), v("pku", 8 * j, 8 * j + 8)), F.Copy)
+    quant(v("qx", 0, 192), v("sx", 0, 192), v("xt", 0, 768))
+    quant(v("qx", 192, 384), v("sx", 192, 384), v("xt", 768, 1536))
+    tt(v("rw", 16, 32), v("rw", 0, 16), v("cmin", 0, 16), A.min)
+    add("v", lambda e: e.tensor_reduce(ap(wt_), ap(v("rw", 16, 32)), AxisListType.X, A.max), [v("rw", 16, 32)], [wt_], 64)
+    ts(v("kt", 0, 512), v("grp"), g_, A.is_equal)
+    quant(v("qk", 0, 128), v("sk", 0, 128), v("kt", 0, 512))
+    cp(v("lu"), v("l32"))
+    cp(v("mu"), v("m32"))
+    ts(r2_, q_, 2.0, A.is_equal)
+    ts(r2b_, q_, 2.0, A.is_equal, -192.0, A.mult)
+    act(v("lm"), ind(v("iot"), v("lu")), F.Identity, bias=r2b_, scale=r2_)
+    act(v("lmb"), ind(v("iot"), v("mu")), F.Identity, bias=-192.0)
+    dma("y", lambda: T.lm[10:128:16, :], lambda: T.lmb[10:128:16, :], [v("lmb")], [v("lm")])
+    act(v("cxw"), ind(v("sm", 384, 512), v("pu")), F.Copy)
+    ts(v("cxw", 15, C, 16), v("cxw", 15, C, 16), -4096.0, A.add)
+    dma("y", lambda: T.cxr[:], lambda: T.cxw[:], [v("cxw")], [v("cxr")])
+    ts(hq_, h_, 16.0, A.mult, q_, A.subtract)
+    ts(v("base"), v("base"), hq_, A.add)
+    tt(v("base"), v("base"), v("cxw", 15, C, 16), A.add)
+    ts(nh_, h_, -1.0, A.mult, 1.0, A.add)
+    ts(junk_, q_, 384.0, A.add)
+    act(v("kt", 1024, 1536), v("ktmp"), F.Identity, scale=nh_)
+    act(v("kt", 1536, 2048), v("ktmp"), F.Identity, scale=h_)
+    for j in range(1, 4):
+        quant(v("qk", 128 * j, 128 * j + 128), v("sk", 128 * j, 128 * j + 128), v("kt", 512 * j, 512 * j + 512))
+    ts(v("m48"), v("m48"), h_, A.is_equal)
+    for b in range(4):
+        quant(v("qe", 128 * b, 128 * b + 128), v("se", 128 * b, 128 * b + 128), v("et", 3 - b, 515 - b))
+    act(v("camp"), ind(v("sm", 512, 640), v("pu", 0, 12)), F.Copy)
+    cp(v("repu"), v("c32"))
+    ms(v("camp", 15, K, 16), 2.0 ** -12)
+    quant(v("qv"), v("sv"), v("vt"))
+
+    def slot(c):
+        for i in range(6):
+            if c in SLOTS[i]:
+                w = 16 * c if c else C
+                a = 4 * TOFF[i] + SLOTS[i].index(c)
+                return v("ct", a, a + 4 * w - 3, 4)
+
+    def kq(i):
+        return v("qk", 128 * i, 128 * i + 128), v("sk", 128 * i, 128 * i + 128)
+
+    def eq_(b):
+        return v("qe", 128 * b, 128 * b + 128), v("se", 128 * b, 128 * b + 128)
+
+    def ym(s):
+        return v("qy", s, s + 128), v("sy", s, s + 128)
+
+    for t in range(R):
+        ub = (v("qu2", 0, 128), v("su2", 0, 128))
+        mm(bank(0, C), ub[0], ub[1], v("qx"), v("sx"))
+        mm(bank(2, C), v("qu2", 128, 256), v("su2", 128, 256), v("qx"), v("sx"))
+        mm(bank(1, C), ub[0], ub[1], v("qx"), v("sx"))
+        for b in range(4):
+            mm(bank(4 + b, C), eq_(b)[0], eq_(b)[1], v("qx"), v("sx"))
+            act(v("tv", 576 * b + K, 576 * b + 576), bank(4 + b, C), F.Copy)
+        tt(v("m1"), bank(0, C), v("cmin"), A.min)
+        scan(v("hh"), v("khold"), v("m1"), -BIG, A.min, A.max)
+        act(v("sgb"), bank(2, C), F.Sign)
+        act(v("bw"), v("sgb"), F.Relu, scale=wt_)
+        tt(v("x1"), ind(v("bw"), v("mu")), v("lm"), A.subtract)
+        tt(v("pay"), ind(v("bw"), v("lu")), v("x1"), A.subtract)
+        tt(slot(0), bank(0, C), v("hh"), A.is_le)
+        scan(v("rd"), v("keep"), slot(0), 0.0, A.min, A.add)
+        tt(v("base2"), v("base"), v("rd", 15, C, 16), A.subtract)
+        for c in range(23, 0, -1):
+            z = c1("hh", 16 * c + 15)
+            if c in S_ROWS[t]:
+                s = v("sg", ROFF[c], ROFF[c + 1])
+                act(s, bank(1, 16 * c), F.Sign, bias=z, scale=-1.0)
+                act(slot(c), s, F.Relu, acc=c1("rs", c))
+            else:
+                ts(slot(c), bank(0, 16 * c), z, A.is_lt)
+                act(v("jk", ROFF[c], ROFF[c + 1]), slot(c), F.Identity, acc=c1("rs", c))
+        for i in range(6):
+            a, w = TOFF[i], TILES[i]
+            quant(v("qc", a, a + w), v("sc", a, a + w), v("ct", 4 * a, 4 * (a + w)))
+            mm(bank(3, w), kq(0)[0], kq(0)[1], v("qc", a, a + w), v("sc", a, a + w), i == 0, i == 5)
+        tt(v("cxr", 15, C, 16), v("base2"), v("rs"), A.subtract)
+        scan(v("xs"), bank(3, C), v("cxr"), -1.0, A.max, A.add)
+        ts(v("rk"), v("xs", 15, C, 16), 3072.0, A.add)
+        cp(ind(v("pw"), v("rk")), v("pay"))
+        turn(v("yt", 0, 192), v("pw", 0, 192))
+        turn(v("yt", 192, 384), v("pw", 16, 208))
+        quant(v("qy"), v("sy"), v("yt"))
+        for j, (ki, s) in enumerate([(2, 0), (2, 2), (3, 4), (3, 6)]):
+            mm(bank(1, 128), kq(ki)[0], kq(ki)[1], ym(s)[0], ym(s)[1], j == 0, j == 3)
+        for j in range(2):
+            mm(bank(0, 128), kq(1)[0], kq(1)[1], ym(2 * j)[0], ym(2 * j)[1], j == 0, j == 1)
+        tt(v("w48"), v("yt", 2, 384, 8), v("m48"), A.mult)
+        tt(v("ab", 0, 12), v("w48", 0, 48, 4), v("w48", 2, 48, 4), A.add)
+        tt(v("ab", 12, 24), v("w48", 1, 48, 4), v("w48", 3, 48, 4), A.add)
+        ts(v("ab2"), v("ab"), 192.0, A.add)
+        tt(v("ee"), v("ab", 12, 24), v("ab", 0, 12), A.subtract)
+        act(v("bs"), bank(1, 96, 1, 8), F.Identity, scale=2.0 ** -12)
+        tt(v("ppi"), bank(0, 96, 0, 8), v("bs"), A.mult)
+        ts(v("fl"), v("ppi"), 3, A.arith_shift_right, 1, A.bitwise_and)
+        tt(v("fe"), v("fl"), v("ee"), A.mult)
+        tt(v("lr", 0, 12), v("ab2", 0, 12), v("fe"), A.add)
+        tt(v("lr", 12, 24), v("ab2", 12, 24), v("fe"), A.subtract)
+        cp(v("lru"), v("lr"))
+        act(v("ff"), ind(v("iot"), v("lru", 0, 12)), F.Copy)
+        for b in range(4):
+            tw = v("tv", 576 * b + K, 576 * b + 576)
+            act(v("ln", K * b, K * b + K), ind(tw, v("lru", 0, 12)), F.Copy)
+            tt(v("mt", b, 4 * K, 4), ind(tw, v("lru", 12, 24)), v("ln", K * b, K * b + K), A.subtract)
+        quant(v("qm"), v("smm"), v("mt"))
+        arrived(t)
+        for b in range(4):
+            mm(bank(4 + b, K), v("wq%d" % t, 128 * b, 128 * b + 128), v("wp%d" % t, 128 * b, 128 * b + 128), v("qm"), v("smm"))
+            act(v("ht", b, 4 * K, 4), bank(4 + b, K), F.Identity, scale=0.03125)
+        quant(v("qh"), v("sh"), v("ht"))
+        for b in range(4):
+            mm(bank(b, K), eq_(b)[0], eq_(b)[1], v("qh"), v("sh"))
+            tt(v("tv", 576 * b, 576 * b + K), bank(b, K), v("ln", K * b, K * b + K), A.add)
+        tt(v("eq"), ind(v("lr", 0, 12), v("repu")), v("ff"), A.is_equal)
+        scan(v("es"), v("eq"), v("camp"), 0.0, A.add, A.mult)
+        ts(v("d1"), v("es", 15, K, 16), 48.0 / 4096.0, A.is_gt, junk_, A.mult)
+        tt(v("d2"), v("d1"), v("lr", 0, 12), A.max)
+        cp(v("du", 0, 24, 2), v("d2"))
+        for c in range(11, -1, -1):
+            s = c // 2 + 6 * (c % 2)
+            cp(ind(v("wh", 400 * t, 400 * t + 400), v("du", 2 * s, 2 * s + 1)), v("iot", 16 * s, 16 * s + 16))
+        scan(v("xw"), v("wh", 400 * t, 400 * t + C), v("cxw"), -1.0, A.max, A.add)
+        ts(v("wu"), v("xw", 15, C, 16), 3072.0, A.add)
+        for b in range(4):
+            w = v("tv", 576 * b, 576 * b + 576)
+            if b < 2:
+                act(v("xt", b, 4 * C, 4), ind(w, v("wu")), F.Identity, scale=-2.0)
+            elif b == 3:
+                ts(v("xt", b, 4 * C, 4), ind(w, v("wu")), -2.0, A.mult)
+            else:
+                act(v("xt", b, 2 * C, 4), ind(w, v("wu", 0, 12)), F.Identity, scale=-2.0)
+                ts(v("xt", 2 * C + b, 4 * C, 4), ind(w, v("wu", 12, 24)), -2.0, A.mult)
+        if t < R - 1:
+            quant(v("qx"), v("sx"), v("xt"))
+
+    cp(v("olu", 0, 12, 2), v("lr", 0, 6))
+    cp(v("olu", 1, 12, 2), v("lr", 6, 12))
+    cp(v("olu", 12, 24, 2), v("lr", 12, 18))
+    cp(v("olu", 13, 24, 2), v("lr", 18, 24))
+    act(v("olf"), ind(v("iot"), v("olu")), F.Copy)
+    dma("y", lambda: T.ol[:], lambda: T.olf[0:128:16, :], [v("olf")], [])
+    for j in range(2):
+        a, b = K * j, K * j + K
+        quant(v("qx", a, b), v("sx", a, b), v("xt", 4 * a, 4 * b))
+        mm(bank(j, K), v("qv"), v("sv"), v("qx", a, b), v("sx", a, b))
+    act(v("yf", 0, K), bank(0, K), F.Copy)
+    cp(v("yf", K, C), bank(1, K))
+    dma("s", lambda: T.y[:, 0:K], lambda: T.yf[:, 0:K], [v("yf", 0, K)], [])
+    dma("s", lambda: T.y[:, K:C], lambda: T.yf[:, K:C], [v("yf", K, C)], [])
+    dma("y", lambda: T.oc[:], lambda: T.qx[:].bitcast(dt.uint8), [v("qx")], [], 3000)
+    for k in range(4):
+        dma("y", lambda k=k: T.osc[4 * k:4 * k + 4, :], lambda k=k: T.sx[32 * k:32 * k + 4, :], [v("sx")], [])
+    return ops
+
+
+def clashes(ops):
+    hist, out = {}, []
+    for i, o in enumerate(ops):
+        deps = {}
+        for ws, w in ((o[2], False), (o[3], True)):
+            for x in ws:
+                m = _mask(x)
+                for (j, mj, wj) in hist.get(x[0], []):
+                    if m & mj and (w or wj or (x[0] == "ps" and ops[j][0] != o[0])):
+                        deps[j] = deps.get(j, False) or (wj and not w)
+        for ws, w in ((o[2], False), (o[3], True)):
+            for x in ws:
+                hist.setdefault(x[0], []).append((i, _mask(x), w))
+        out.append(deps)
+    return out
+
+
+def inline(a, b, raw):
+    return a[0] == b[0] and a[4] in ("c", "w") and b[4] in ("c", "w") and (a[0] == "p" or not (raw or SAMEQ))
+
+
+def plan(ops):
+    deps, n = clashes(ops), len(ops)
+    after = [[] for o in ops]
+    for i in range(n):
+        for j in deps[i]:
+            after[j].append(i)
+    lag = [dict((j, 0.0 if inline(ops[j], ops[i], deps[i][j]) else WAKE) for j in deps[i]) for i in range(n)]
+    ns, qs = [o[5] for o in ops], [o[0] for o in ops]
+    hold = [o[5] if o[4] in ("c", "w") else 60.0 if o[4] == "d" else 500.0 for o in ops]
+    for chain in ([i for i in range(n) if qs[i] == "y" and not ops[i][2]], [i for i in range(n) if qs[i] == "g"]):
+        for j, i in zip(chain, chain[1:]):
+            if j not in deps[i]:
+                deps[i][j] = False
+                lag[i][j] = hold[j] - ns[j]
+                after[j].append(i)
+    tail = [0.0] * n
+    for i in range(n - 1, -1, -1):
+        tail[i] = ns[i] + max([0.0] + [lag[k][i] + tail[k] for k in after[i]])
+    pre = [[(j, ns[j] + lag[i][j]) for j in deps[i]] for i in range(n)]
+
+    def lay(key):
+        busy, start, left = dict((q, []) for q in "vspgy"), [0.0] * n, [len(d) for d in deps]
+        ready = sorted((key[i], i) for i in range(n) if not left[i])
+        while ready:
+            i = ready.pop(0)[1]
+            s = 0.0
+            for j, d in pre[i]:
+                if start[j] + d > s:
+                    s = start[j] + d
+            b, h = busy[qs[i]], hold[i]
+            k = len(b)
+            while k and b[k - 1][1] > s:
+                k -= 1
+            while k < len(b) and s + h > b[k][0]:
+                s = max(s, b[k][1])
+                k += 1
+            b.insert(k, (s, s + h))
+            start[i] = s
+            new = False
+            for k in after[i]:
+                left[k] -= 1
+                if not left[k]:
+                    ready.append((key[k], k))
+                    new = True
+            if new:
+                ready.sort()
+        return max(start[i] + ns[i] for i in range(n)), start
+
+    best = lay([-x for x in tail])
+    rng = np.random.RandomState(1)
+    for _ in range(PASSES):
+        mid, wide, sd = rng.uniform(0, best[0]), rng.uniform(500, 3000), rng.choice([300.0, 1000.0, 3000.0])
+        k2 = [best[1][i] + (sd * float(rng.randn()) if abs(best[1][i] - mid) < wide and rng.rand() < 0.15 else 0.0) for i in range(n)]
+        got = lay(k2)
+        if got[0] <= best[0]:
+            best = got
+    return sorted(range(n), key=lambda k: (best[1][k], k))
+
+
+def order(ops):
+    deps, waits, clock = clashes(ops), [], []
+    known = dict((q, set()) for q in "vspgy")
+    mine = dict((q, set()) for q in "vspgy")
+    for i, o in enumerate(ops):
+        need = []
+        for j in sorted(deps[i], reverse=True):
+            if j not in known[o[0]] and ops[j][4] in ("c", "d") and o[4] != "w" and not inline(ops[j], o, deps[i][j]):
+                need.append(j)
+                known[o[0]] |= clock[j]
+        waits.append(need)
+        if o[4] == "c":
+            mine[o[0]].add(i)
+            clock.append(known[o[0]] | mine[o[0]])
+        else:
+            clock.append(known[o[0]] | set([i]))
+    return waits
+
+
+LAID = []
+
+
+def rank_program(g, core, T, topo):
+    if T.rank_of(core) is None:
+        return
+    ops = build(T, topo, core)
+    if not LAID:
+        seq = plan(ops)
+        LAID.extend([seq, order([ops[i] for i in seq])])
+    ops, waits = [ops[i] for i in LAID[0]], LAID[1]
+    eng = {"v": g.vector, "s": g.scalar, "p": g.tensor, "g": g, "y": g.sync}
+    needed = set(j for w in waits for j in w)
+    where, count, ndma, sent, open_dma = {}, dict((q, 0) for q in CSEM), 0, 0, []
+    for i, (q, fn, rd, wr, kind, ns) in enumerate(ops):
+        for j in waits[i]:
+            eng[q].wait_ge(where[j][0], where[j][1])
+        r = fn(eng[q])
+        if kind == "d":
+            where[i] = (T.sem["d%d" % ndma], 16)
+            ndma += 1
+            r.then_inc(where[i][0], 16)
+            if i not in needed:
+                open_dma.append(i)
+        elif kind == "c" and i in needed:
+            count[q] += 1
+            where[i] = (T.sem[CSEM[q]], count[q])
+            r.then_inc(where[i][0], 1)
+        elif isinstance(kind, tuple):
+            sent += kind[1]
+    g.wait_ge(T.sem.sent, sent)
+    for i in open_dma:
+        g.sync.wait_ge(where[i][0], 16)

@@ -10,11 +10,10 @@ WIDE = {BF: 2, F32: 4, I32: 4, U16: 2, Q4: 4, U8: 1}
 TILES = [384, 320, 256, 192, 128, 128]
 SLOTS = [[0, 23, 22, 21], [20, 19, 18, 17], [16, 15, 14, 13], [12, 11, 10, 9], [8, 7, 6, 5], [4, 3, 2, 1]]
 TOFF = [sum(TILES[:i]) for i in range(6)]
-S_ROWS = [(23, 22), (23, 22), (23, 22)]
+S_ROWS = (23, 22)
 ROFF = [8 * c * (c - 1) for c in range(25)]
-SAMEQ = True
-CY, PE, GAT, SCA, WAKE = 1.0, 0.6, 1.5, 3.5, 80.0
-PASSES = 7000
+CY, PE, GAT, SCA, WAKE = 0.9, 0.6, 1.5, 3.5, 110.0
+PASSES = 8000
 
 
 def _sb(n, d):
@@ -29,23 +28,24 @@ SCRATCH = {
     "wq0": _sb(512, Q4), "wp0": _sb(512, U8), "wq1": _sb(512, Q4), "wp1": _sb(512, U8), "wq2": _sb(512, Q4), "wp2": _sb(512, U8),
     "l32": _sb(24, I32), "m32": _sb(24, I32), "lu": _sb(24, U16), "mu": _sb(24, U16),
     "half": _sb(516, BF), "et": _sb(516, BF), "qe": _sb(512, Q4), "se": _sb(512, U8),
-    "grp": _sb(512, BF), "one01": _sb(512, BF), "ktmp": _sb(512, BF), "kt": _sb(2048, BF), "qk": _sb(512, Q4), "sk": _sb(512, U8),
+    "grp": _sb(512, BF), "c12": _sb(512, BF), "byh": _sb(512, BF), "ktmp": _sb(512, BF), "kt": _sb(1024, BF), "qk": _sb(256, Q4), "sk": _sb(256, U8),
+    "kb": _sb(48, F32), "w1": _sb(48, F32), "b48": _sb(48, F32),
     "ct": _sb(4 * 1408, BF), "qc": _sb(1408, Q4), "sc": _sb(1408, U8),
     "jk": _sb(4416, BF), "sg": _sb(4416, BF),
     "cin": _sb(3 * 128, F32), "sm": _sb(5 * 128, F32),
-    "p32": _sb(24, I32), "pu": _sb(24, U16), "c32": _sb(12, I32), "repu": _sb(12, U16),
+    "p32": _sb(24, I32), "pu": _sb(24, U16), "c32": _sb(18, I32), "repu": _sb(18, U16),
     "pi": _sb(8, I32), "col": _sb(16, F32), "pk32": _sb(16, I32), "pkf": _sb(8, F32), "pku": _sb(16, U16),
-    "cmin": _sb(C, F32), "khold": _sb(C, F32), "cxr": _sb(C, F32), "cxw": _sb(C, F32), "camp": _sb(K, F32), "keep": _sb(C, BF),
+    "cmin": _sb(C, F32), "khold": _sb(C, F32), "cxr": _sb(C, F32), "cxw": _sb(C, F32), "camp": _sb(288, F32), "keep": _sb(C, BF),
     "rw": _sb(32, F32), "base": _sb(24, F32), "base2": _sb(24, F32), "m48": _sb(48, F32),
-    "iot": _sb(C, F32), "lmb": _sb(C, F32), "lm": _sb(C, F32), "wh": _sb(3 * 400, F32),
+    "iot": _sb(C, F32), "lmb": _sb(C, F32), "lm": _sb(C, F32), "wh": _sb(3 * 416, F32), "kv": _sb(K, F32),
     "m1": _sb(C, F32), "hh": _sb(C, F32), "rd": _sb(C, BF), "rs": _sb(24, F32), "xs": _sb(C, F32), "rk": _sb(24, U16),
     "sgb": _sb(C, BF), "bw": _sb(C, BF), "x1": _sb(C, F32), "pay": _sb(C, BF), "pw": _sb(416, BF),
     "yt": _sb(544, BF), "qy": _sb(136, Q4), "sy": _sb(136, U8),
-    "w48": _sb(48, F32), "ab": _sb(24, F32), "ab2": _sb(24, F32), "ee": _sb(12, F32), "bs": _sb(12, F32),
+    "w48": _sb(48, F32), "ab": _sb(24, F32), "ab2": _sb(24, F32), "ee": _sb(12, F32),
     "ppi": _sb(12, I32), "fl": _sb(12, I32), "fe": _sb(12, F32), "lr": _sb(24, F32), "lru": _sb(24, U16),
     "tv": _sb(4 * 576, BF), "ln": _sb(4 * K, BF), "mt": _sb(4 * K, BF), "qm": _sb(K, Q4), "smm": _sb(K, U8),
     "ht": _sb(4 * K, BF), "qh": _sb(K, Q4), "sh": _sb(K, U8),
-    "ff": _sb(K, F32), "eq": _sb(K, F32), "es": _sb(K, F32), "d1": _sb(12, F32), "d2": _sb(12, F32), "du": _sb(24, U16),
+    "ff": _sb(288, F32), "eq": _sb(288, F32), "es": _sb(288, F32), "d1": _sb(12, F32), "d2": _sb(12, F32), "du": _sb(12, U16),
     "xw": _sb(C, F32), "wu": _sb(24, U16), "olu": _sb(24, U16), "olf": _sb(C, F32), "yf": _sb(C, F32),
     "ps": ("psum", [128, 4096], F32),
 }
@@ -175,21 +175,21 @@ def build(T, topo, core):
 
     rank = T.rank_of(core)
     n = len(T.cores)
+    dst, src = T.cores[(rank - 1) % n], T.cores[(rank + 1) % n]
+    rid, pid, emask = topo.addr(dst)[0], topo.addr(dst)[1], topo.mask(core, dst)
+    nout, nin = len(topo.engines(core, dst)), 2 * len(topo.engines(src, core))
 
     def send(t):
-        dst = T.cores[(rank - 1 - t) % n]
-        rid, pid = topo.addr(dst)[0], topo.addr(dst)[1]
-        m = topo.mask(core, dst)
-        cnt = len(topo.engines(core, dst))
-        add("g", lambda e: e.remote_dma(ap(v("wq%d" % t), dt.uint8), ap(v("wq"), dt.uint8), T.sem["arr%d" % t], T.sem.sent, pid, rid, m),
-            [v("wq")], [v("wq%d" % t, 0, 1)], 9000, ("r", cnt))
-        add("g", lambda e: e.remote_dma(ap(v("wp%d" % t)), ap(v("wp")), T.sem["arr%d" % t], T.sem.sent, pid, rid, m),
-            [v("wp")], [v("wp%d" % t, 0, 1)], 9000, ("r", cnt))
+        q, s = ("wq%d" % (t - 1), "wp%d" % (t - 1)) if t else ("wq", "wp")
+        if t:
+            add("g", lambda e: e.wait_ge(T.sem["arr%d" % (t - 1)], nin), [v(q, 0, 1), v(s, 0, 1)], [], 1, "w")
+        add("g", lambda e: e.remote_dma(ap(v("wq%d" % t), dt.uint8), ap(v(q), dt.uint8), T.sem["arr%d" % t], T.sem.sent, pid, rid, emask),
+            [v(q, 0, 1)], [v("wq%d" % t, 0, 1)], 9000, ("r", nout))
+        add("g", lambda e: e.remote_dma(ap(v("wp%d" % t)), ap(v(s)), T.sem["arr%d" % t], T.sem.sent, pid, rid, emask),
+            [v(s, 0, 1)], [v("wp%d" % t, 0, 1)], 9000, ("r", nout))
 
     def arrived(t):
-        src = T.cores[(rank + 1 + t) % n]
-        cnt = 2 * len(topo.engines(src, core))
-        add("p", lambda e: e.wait_ge(T.sem["arr%d" % t], cnt), [v("qm")], [v("wq%d" % t), v("wp%d" % t)], 1, "w")
+        add("p", lambda e: e.wait_ge(T.sem["arr%d" % t], nin), [v("qm")], [v("wq%d" % t, 2, 512), v("wp%d" % t, 2, 512)], 1, "w")
 
     def c1(name, j):
         return v(name, j, j + 1)
@@ -207,6 +207,7 @@ def build(T, topo, core):
     ms(v("cin", 128, 256), 1024.0)
     ms(v("cin", 256, 384), 64.0)
     ms(v("half"), -0.5)
+    ms(v("c12"), 2.0 ** -12)
     iota(v("p32"), [[0, 24]], 0, 1)
     sel(v("sm", 0, 128), v("cin", 0, 128), [[1, 128]], A.is_equal, -BIG, 0, -1)
     sel(v("sm", 128, 256), v("cin", 0, 128), [[1, 128]], A.is_gt, -BIG, 0, -1)
@@ -219,16 +220,18 @@ def build(T, topo, core):
     sel(v("sm", 384, 512), v("sm", 256, 384), [[1, 128]], A.is_ge, -4096.0, 0, -1)
     iota(v("base"), [[16, 24]], 15, 0)
     sel(v("et"), v("half"), [[-1, 516]], A.is_equal, 0.0, 3, 4)
-    iota(v("one01"), [[0, 128], [-1, 2], [0, 2]], 1, 0)
-    sel(v("kt", 512, 1024), v("one01"), [[0, 8], [-1, 16], [0, 4]], A.is_equal, 0.0, 0, 1)
-    sel(v("ktmp"), v("one01"), [[-1, 128], [0, 4]], A.is_equal, 0.0, 0, 1)
+    sel(v("byh"), v("c12"), [[0, 4], [1, 2], [0, 64]], A.is_gt, 2.0 ** -28, 0, 0)
+    sel(v("ktmp"), v("byh"), [[0, 128], [1, 2], [0, 2]], A.is_equal, 0.0, 0, 0)
+    sel(v("kt", 512, 1024), v("ktmp"), [[0, 8], [-1, 16], [0, 4]], A.is_equal, 0.0, 0, 1)
     iota(v("m48"), [[0, 12], [1, 2], [0, 2]], 0, 0)
     sel(v("sm", 512, 640), v("cin", 256, 384), [[1, 128]], A.is_equal, 1.0, 1, -1)
-    iota(v("c32"), [[1, 12]], 0, 0)
-    iota(v("wh", 0, 400), [[1, 400]], K, 0)
+    iota(v("c32", 0, 12), [[1, 12]], 0, 0)
+    iota(v("c32", 12, 18), [[1, 6]], 6, 0)
+    iota(v("kv"), [[16, 6], [96, 2], [1, 16]], 0, 0)
+    iota(v("wh", 0, 416), [[1, 416]], K, 0)
+    iota(v("wh", 416, 1248), [[0, 2], [1, 416]], K, 0)
     send(1)
     send(2)
-    iota(v("wh", 400, 1200), [[0, 2], [1, 400]], K, 0)
 
     cp(v("pu"), v("p32"))
     ts(c1("pi", 0), c1("p32", 0), 1, A.bitwise_and)
@@ -237,7 +240,7 @@ def build(T, topo, core):
     ts(c1("pi", 3), c1("p32", 0), 4, A.logical_shift_right, 1, A.bitwise_and)
     ts(c1("pi", 4), c1("p32", 0), 4, A.logical_shift_right)
     cp(v("col", 0, 5), v("pi", 0, 5))
-    q_, h_, g_, wt_, r2_, r2b_, hq_, nh_, junk_ = [c1("col", j) for j in range(2, 11)]
+    q_, h_, g_, wt_, r2_, r2b_, hq_, nh_, junk_, junk2_ = [c1("col", j) for j in range(2, 12)]
     cp(v("pku", 0, 8), v("pk32", 0, 8))
     ts(v("pkf"), v("pk32", 8, 16), c1("col", 0), A.add, c1("col", 1), A.add)
     ts(v("pku", 8, 16), v("pkf"), 1.0, A.add)
@@ -278,14 +281,17 @@ def build(T, topo, core):
     tt(v("base"), v("base"), v("cxw", 15, C, 16), A.add)
     ts(nh_, h_, -1.0, A.mult, 1.0, A.add)
     ts(junk_, q_, 384.0, A.add)
-    act(v("kt", 1024, 1536), v("ktmp"), F.Identity, scale=nh_)
-    act(v("kt", 1536, 2048), v("ktmp"), F.Identity, scale=h_)
-    for j in range(1, 4):
-        quant(v("qk", 128 * j, 128 * j + 128), v("sk", 128 * j, 128 * j + 128), v("kt", 512 * j, 512 * j + 512))
+    ts(junk2_, q_, 400.0, A.add)
+    quant(v("qk", 128, 256), v("sk", 128, 256), v("kt", 512, 1024))
+    ms(v("kb"), 1.0)
+    ms(v("kb", 0, 48, 4), 0.0)
+    ts(v("kb", 2, 48, 4), v("kb", 1, 48, 4), nh_, A.mult, 65536.0, A.mult)
     ts(v("m48"), v("m48"), h_, A.is_equal)
     for b in range(4):
         quant(v("qe", 128 * b, 128 * b + 128), v("se", 128 * b, 128 * b + 128), v("et", 3 - b, 515 - b))
-    act(v("camp"), ind(v("sm", 512, 640), v("pu", 0, 12)), F.Copy)
+    ms(v("camp", K, 288), 1.0)
+    ms(v("camp", K + 15, 288, 16), 2.0 ** -6)
+    act(v("camp", 0, K), ind(v("sm", 512, 640), v("pu", 0, 12)), F.Copy)
     cp(v("repu"), v("c32"))
     ms(v("camp", 15, K, 16), 2.0 ** -12)
     quant(v("qv"), v("sv"), v("vt"))
@@ -325,7 +331,7 @@ def build(T, topo, core):
         tt(v("base2"), v("base"), v("rd", 15, C, 16), A.subtract)
         for c in range(23, 0, -1):
             z = c1("hh", 16 * c + 15)
-            if c in S_ROWS[t]:
+            if c in S_ROWS:
                 s = v("sg", ROFF[c], ROFF[c + 1])
                 act(s, bank(1, 16 * c), F.Sign, bias=z, scale=-1.0)
                 act(slot(c), s, F.Relu, acc=c1("rs", c))
@@ -343,8 +349,8 @@ def build(T, topo, core):
         turn(v("yt", 0, 192), v("pw", 0, 192))
         turn(v("yt", 192, 384), v("pw", 16, 208))
         quant(v("qy"), v("sy"), v("yt"))
-        for j, (ki, s) in enumerate([(2, 0), (2, 2), (3, 4), (3, 6)]):
-            mm(bank(1, 128), kq(ki)[0], kq(ki)[1], ym(s)[0], ym(s)[1], j == 0, j == 3)
+        tt(v("w1"), v("yt", 4, 384, 8), v("yt", 5, 384, 8), A.add)
+        scan(v("b48"), v("kb"), v("w1"), 0.0, A.mult, A.add)
         for j in range(2):
             mm(bank(0, 128), kq(1)[0], kq(1)[1], ym(2 * j)[0], ym(2 * j)[1], j == 0, j == 1)
         tt(v("w48"), v("yt", 2, 384, 8), v("m48"), A.mult)
@@ -352,14 +358,14 @@ def build(T, topo, core):
         tt(v("ab", 12, 24), v("w48", 1, 48, 4), v("w48", 3, 48, 4), A.add)
         ts(v("ab2"), v("ab"), 192.0, A.add)
         tt(v("ee"), v("ab", 12, 24), v("ab", 0, 12), A.subtract)
-        act(v("bs"), bank(1, 96, 1, 8), F.Identity, scale=2.0 ** -12)
-        tt(v("ppi"), bank(0, 96, 0, 8), v("bs"), A.mult)
+        tt(v("ppi"), bank(0, 96, 0, 8), v("b48", 3, 48, 4), A.mult)
         ts(v("fl"), v("ppi"), 3, A.arith_shift_right, 1, A.bitwise_and)
         tt(v("fe"), v("fl"), v("ee"), A.mult)
         tt(v("lr", 0, 12), v("ab2", 0, 12), v("fe"), A.add)
         tt(v("lr", 12, 24), v("ab2", 12, 24), v("fe"), A.subtract)
         cp(v("lru"), v("lr"))
-        act(v("ff"), ind(v("iot"), v("lru", 0, 12)), F.Copy)
+        act(v("ff", 0, K), ind(v("iot"), v("lru", 0, 12)), F.Copy)
+        act(v("ff", K, 288), ind(v("iot"), v("lru", 0, 6)), F.Copy)
         for b in range(4):
             tw = v("tv", 576 * b + K, 576 * b + 576)
             act(v("ln", K * b, K * b + K), ind(tw, v("lru", 0, 12)), F.Copy)
@@ -375,13 +381,15 @@ def build(T, topo, core):
             tt(v("tv", 576 * b, 576 * b + K), bank(b, K), v("ln", K * b, K * b + K), A.add)
         tt(v("eq"), ind(v("lr", 0, 12), v("repu")), v("ff"), A.is_equal)
         scan(v("es"), v("eq"), v("camp"), 0.0, A.add, A.mult)
-        ts(v("d1"), v("es", 15, K, 16), 48.0 / 4096.0, A.is_gt, junk_, A.mult)
+        tt(v("es", 111, K, 16), v("es", 111, K, 16), v("es", K + 15, 288, 16), A.max)
+        ts(v("d1", 0, 6), v("es", 15, 96, 16), 48.0 / 4096.0, A.is_gt, junk_, A.mult)
+        ts(v("d1", 6, 12), v("es", 111, K, 16), 48.0 / 4096.0, A.is_gt, junk2_, A.mult)
         tt(v("d2"), v("d1"), v("lr", 0, 12), A.max)
-        cp(v("du", 0, 24, 2), v("d2"))
-        for c in range(11, -1, -1):
-            s = c // 2 + 6 * (c % 2)
-            cp(ind(v("wh", 400 * t, 400 * t + 400), v("du", 2 * s, 2 * s + 1)), v("iot", 16 * s, 16 * s + 16))
-        scan(v("xw"), v("wh", 400 * t, 400 * t + C), v("cxw"), -1.0, A.max, A.add)
+        cp(v("du", 0, 12, 2), v("d2", 0, 6))
+        cp(v("du", 1, 12, 2), v("d2", 6, 12))
+        for c in range(5, -1, -1):
+            cp(ind(v("wh", 416 * t, 416 * t + 416), v("du", 2 * c, 2 * c + 2)), v("kv", 32 * c, 32 * c + 32))
+        scan(v("xw"), v("wh", 416 * t, 416 * t + C), v("cxw"), -1.0, A.max, A.add)
         ts(v("wu"), v("xw", 15, C, 16), 3072.0, A.add)
         for b in range(4):
             w = v("tv", 576 * b, 576 * b + 576)
@@ -405,11 +413,11 @@ def build(T, topo, core):
         a, b = K * j, K * j + K
         quant(v("qx", a, b), v("sx", a, b), v("xt", 4 * a, 4 * b))
         mm(bank(j, K), v("qv"), v("sv"), v("qx", a, b), v("sx", a, b))
+        dma("y", lambda a=a, b=b: T.oc[:, 4 * a:4 * b], lambda a=a, b=b: T.qx[:, a:b].bitcast(dt.uint8), [v("qx", a, b)], [], 2700)
     act(v("yf", 0, K), bank(0, K), F.Copy)
     cp(v("yf", K, C), bank(1, K))
     dma("s", lambda: T.y[:, 0:K], lambda: T.yf[:, 0:K], [v("yf", 0, K)], [])
     dma("s", lambda: T.y[:, K:C], lambda: T.yf[:, K:C], [v("yf", K, C)], [])
-    dma("y", lambda: T.oc[:], lambda: T.qx[:].bitcast(dt.uint8), [v("qx")], [], 3000)
     for k in range(4):
         dma("y", lambda k=k: T.osc[4 * k:4 * k + 4, :], lambda k=k: T.sx[32 * k:32 * k + 4, :], [v("sx")], [])
     return ops
@@ -424,7 +432,7 @@ def clashes(ops):
                 m = _mask(x)
                 for (j, mj, wj) in hist.get(x[0], []):
                     if m & mj and (w or wj or (x[0] == "ps" and ops[j][0] != o[0])):
-                        deps[j] = deps.get(j, False) or (wj and not w)
+                        deps[j] = True
         for ws, w in ((o[2], False), (o[3], True)):
             for x in ws:
                 hist.setdefault(x[0], []).append((i, _mask(x), w))
@@ -432,8 +440,8 @@ def clashes(ops):
     return out
 
 
-def inline(a, b, raw):
-    return a[0] == b[0] and a[4] in ("c", "w") and b[4] in ("c", "w") and (a[0] == "p" or not (raw or SAMEQ))
+def inline(a, b):
+    return a[0] == b[0] == "p"
 
 
 def plan(ops):
@@ -442,13 +450,13 @@ def plan(ops):
     for i in range(n):
         for j in deps[i]:
             after[j].append(i)
-    lag = [dict((j, 0.0 if inline(ops[j], ops[i], deps[i][j]) else WAKE) for j in deps[i]) for i in range(n)]
+    lag = [dict((j, 0.0 if inline(ops[j], ops[i]) else WAKE) for j in deps[i]) for i in range(n)]
     ns, qs = [o[5] for o in ops], [o[0] for o in ops]
     hold = [o[5] if o[4] in ("c", "w") else 60.0 if o[4] == "d" else 500.0 for o in ops]
     for chain in ([i for i in range(n) if qs[i] == "y" and not ops[i][2]], [i for i in range(n) if qs[i] == "g"]):
         for j, i in zip(chain, chain[1:]):
             if j not in deps[i]:
-                deps[i][j] = False
+                deps[i][j] = True
                 lag[i][j] = hold[j] - ns[j]
                 after[j].append(i)
     tail = [0.0] * n
@@ -502,7 +510,7 @@ def order(ops):
     for i, o in enumerate(ops):
         need = []
         for j in sorted(deps[i], reverse=True):
-            if j not in known[o[0]] and ops[j][4] in ("c", "d") and o[4] != "w" and not inline(ops[j], o, deps[i][j]):
+            if j not in known[o[0]] and ops[j][4] in ("c", "d") and o[4] != "w" and not inline(ops[j], o):
                 need.append(j)
                 known[o[0]] |= clock[j]
         waits.append(need)

@@ -9,10 +9,19 @@ BF, F32, I32, U16, Q4, U8 = "bfloat16", "float32", "int32", "uint16", "float8_e4
 WIDE = {BF: 2, F32: 4, I32: 4, U16: 2, Q4: 4, U8: 1}
 TILES = [384, 320, 256, 192, 128, 128]
 SLOTS = [[0, 23, 22, 21], [20, 19, 18, 17], [16, 15, 14, 13], [12, 11, 10, 9], [8, 7, 6, 5], [4, 3, 2, 1]]
-TOFF = [sum(TILES[:i]) for i in range(6)]
-S_ROWS = (23, 22)
+TOFF = [0, 384, 704, 1088, 1280, 1408]
+NPAIR = 9
+SUMS = [(2, 0, 0, 128, 2, [(7, 0, 128)]), (2, 1, 0, 128, 2, [(6, 0, 128)]), (3, 0, -64, 128, 2, [(5, 0, 128)]),
+        (3, 1, -64, 128, 2, [(4, 0, 128)]), (4, 0, 0, 256, 1, [(3, 0, 128), (1, 128, 64)]),
+        (4, 1, 0, 256, 1, [(2, 0, 128), (0, 128, 32)]), (1, 1, 0, 144, 2, [(8, 0, 144)]), (1, 0, 0, 160, 2, [(9, 0, 160)])]
+SUMBANK = [4, 5, 6, 7, 2, 4, 5, 6]
+ROUND = 1.5 * 2.0 ** 32
+XT_S = (24, 24, 6, 0)
+HT_V = (1, 3)
+APART = 32768
+TINY = 2.0 ** -110
 ROFF = [8 * c * (c - 1) for c in range(25)]
-CY, PE, GAT, SCA, WAKE = 0.9, 0.6, 1.5, 3.5, 110.0
+CY, PE, GAT, SCA, WAKE = 0.85, 0.6, 1.5, 3.5, 180.0
 PASSES = 8000
 
 
@@ -28,24 +37,25 @@ SCRATCH = {
     "wq0": _sb(512, Q4), "wp0": _sb(512, U8), "wq1": _sb(512, Q4), "wp1": _sb(512, U8), "wq2": _sb(512, Q4), "wp2": _sb(512, U8),
     "l32": _sb(24, I32), "m32": _sb(24, I32), "lu": _sb(24, U16), "mu": _sb(24, U16),
     "half": _sb(516, BF), "et": _sb(516, BF), "qe": _sb(512, Q4), "se": _sb(512, U8),
-    "grp": _sb(512, BF), "c12": _sb(512, BF), "byh": _sb(512, BF), "ktmp": _sb(512, BF), "kt": _sb(1024, BF), "qk": _sb(256, Q4), "sk": _sb(256, U8),
+    "grp": _sb(512, BF), "byh": _sb(512, BF), "kt": _sb(1024, BF), "qk": _sb(256, Q4), "sk": _sb(256, U8),
     "kb": _sb(48, F32), "w1": _sb(48, F32), "b48": _sb(48, F32),
-    "ct": _sb(4 * 1408, BF), "qc": _sb(1408, Q4), "sc": _sb(1408, U8),
-    "jk": _sb(4416, BF), "sg": _sb(4416, BF),
+    "ct": _sb(4 * 1536, BF), "qc": _sb(1536, Q4), "sc": _sb(1536, U8),
+    "jk": _sb(1600, F32), "sg": _sb(4416, BF), "two": _sb(516, BF), "kr": _sb(516, BF), "qr": _sb(256, Q4), "sr": _sb(256, U8),
+    "pp": _sb(10, F32), "ph": _sb(10, F32), "ph2": _sb(10, F32),
     "cin": _sb(3 * 128, F32), "sm": _sb(5 * 128, F32),
-    "p32": _sb(24, I32), "pu": _sb(24, U16), "c32": _sb(18, I32), "repu": _sb(18, U16),
+    "p32": _sb(24, I32), "pu": _sb(24, U16), "c32": _sb(12, I32), "repu": _sb(12, U16),
     "pi": _sb(8, I32), "col": _sb(16, F32), "pk32": _sb(16, I32), "pkf": _sb(8, F32), "pku": _sb(16, U16),
-    "cmin": _sb(C, F32), "khold": _sb(C, F32), "cxr": _sb(C, F32), "cxw": _sb(C, F32), "camp": _sb(288, F32), "keep": _sb(C, BF),
-    "rw": _sb(32, F32), "base": _sb(24, F32), "base2": _sb(24, F32), "m48": _sb(48, F32),
-    "iot": _sb(C, F32), "lmb": _sb(C, F32), "lm": _sb(C, F32), "wh": _sb(3 * 416, F32), "kv": _sb(K, F32),
+    "cmin": _sb(C, F32), "khold": _sb(C, F32), "cxr": _sb(C, F32), "camp": _sb(C, F32), "keep": _sb(C, BF),
+    "rw": _sb(96, F32), "base": _sb(24, F32), "base2": _sb(24, F32), "pk": _sb(24, F32), "pko": _sb(72, F32),
+    "iot": _sb(C, F32), "stair": _sb(C, F32), "wh": _sb(2048, F32), "kv": _sb(K, F32),
     "m1": _sb(C, F32), "hh": _sb(C, F32), "rd": _sb(C, BF), "rs": _sb(24, F32), "xs": _sb(C, F32), "rk": _sb(24, U16),
-    "sgb": _sb(C, BF), "bw": _sb(C, BF), "x1": _sb(C, F32), "pay": _sb(C, BF), "pw": _sb(416, BF),
+    "sgb": _sb(C, BF), "bw": _sb(C, F32), "x1": _sb(C, F32), "pay": _sb(C, BF), "pw": _sb(416, BF),
     "yt": _sb(544, BF), "qy": _sb(136, Q4), "sy": _sb(136, U8),
-    "w48": _sb(48, F32), "ab": _sb(24, F32), "ab2": _sb(24, F32), "ee": _sb(12, F32),
+    "ab2": _sb(24, F32), "ee": _sb(12, F32),
     "ppi": _sb(12, I32), "fl": _sb(12, I32), "fe": _sb(12, F32), "lr": _sb(24, F32), "lru": _sb(24, U16),
     "tv": _sb(4 * 576, BF), "ln": _sb(4 * K, BF), "mt": _sb(4 * K, BF), "qm": _sb(K, Q4), "smm": _sb(K, U8),
     "ht": _sb(4 * K, BF), "qh": _sb(K, Q4), "sh": _sb(K, U8),
-    "ff": _sb(288, F32), "eq": _sb(288, F32), "es": _sb(288, F32), "d1": _sb(12, F32), "d2": _sb(12, F32), "du": _sb(12, U16),
+    "ff": _sb(K, F32), "eq": _sb(C, F32), "es": _sb(C, F32), "du": _sb(12, U16),
     "xw": _sb(C, F32), "wu": _sb(24, U16), "olu": _sb(24, U16), "olf": _sb(C, F32), "yf": _sb(C, F32),
     "ps": ("psum", [128, 4096], F32),
 }
@@ -203,34 +213,39 @@ def build(T, topo, core):
     dma("y", lambda: T.wp[:], lambda: T.ws[:], [], [v("wp")], 4000)
     dma("y", lambda: T.vt[:], lambda: T.v[:], [], [v("vt")])
 
+    def aff(o, i, scale, bias):
+        act(o, i, F.Identity, bias=bias, scale=scale)
+
     ms(v("cin", 0, 128), BIG)
-    ms(v("cin", 128, 256), 1024.0)
-    ms(v("cin", 256, 384), 64.0)
-    ms(v("half"), -0.5)
-    ms(v("c12"), 2.0 ** -12)
+    ms(v("two"), 0.0)
+    quant(v("qc", 960, 1088), v("sc", 960, 1088), v("two", 0, 512))
+    aff(v("half"), v("two"), 1.0, -0.5)
+    aff(v("two", 2, 516, 4), v("two", 2, 516, 4), 1.0, 1.0)
+    aff(v("two", 3, 516, 4), v("two", 3, 516, 4), 1.0, 512.0)
+    aff(v("cin", 128, 256), v("cin", 0, 128), 0.0, 1024.0)
+    aff(v("cin", 256, 384), v("cin", 0, 128), 0.0, 2.0)
     iota(v("p32"), [[0, 24]], 0, 1)
     sel(v("sm", 0, 128), v("cin", 0, 128), [[1, 128]], A.is_equal, -BIG, 0, -1)
     sel(v("sm", 128, 256), v("cin", 0, 128), [[1, 128]], A.is_gt, -BIG, 0, -1)
     iota(v("pk32"), [[0, 2], [16, 8]], 0, 0)
-    iota(v("iot"), [[1, C]], 0, 0)
     iota(v("grp"), [[1, 8], [0, 64]], 0, 0)
-    iota(v("keep"), [[0, 24], [64, 16]], 0, 0)
-    send(0)
+    sel(v("kr"), v("two"), [[-1, 129], [0, 4]], A.is_equal, 0.0, 0, 1)
+    iota(v("iot"), [[1, C]], 0, 0)
     sel(v("sm", 256, 384), v("cin", 128, 256), [[1, 128]], A.is_equal, 0.0, 0, -1)
-    sel(v("sm", 384, 512), v("sm", 256, 384), [[1, 128]], A.is_ge, -4096.0, 0, -1)
     iota(v("base"), [[16, 24]], 15, 0)
+    sel(v("sm", 384, 512), v("sm", 256, 384), [[1, 128]], A.is_ge, -4096.0, 0, -1)
+    ms(v("keep"), 64.0)
+    ms(v("keep", 0, C, 16), 0.0)
     sel(v("et"), v("half"), [[-1, 516]], A.is_equal, 0.0, 3, 4)
-    sel(v("byh"), v("c12"), [[0, 4], [1, 2], [0, 64]], A.is_gt, 2.0 ** -28, 0, 0)
-    sel(v("ktmp"), v("byh"), [[0, 128], [1, 2], [0, 2]], A.is_equal, 0.0, 0, 0)
-    sel(v("kt", 512, 1024), v("ktmp"), [[0, 8], [-1, 16], [0, 4]], A.is_equal, 0.0, 0, 1)
-    iota(v("m48"), [[0, 12], [1, 2], [0, 2]], 0, 0)
-    sel(v("sm", 512, 640), v("cin", 256, 384), [[1, 128]], A.is_equal, 1.0, 1, -1)
-    iota(v("c32", 0, 12), [[1, 12]], 0, 0)
-    iota(v("c32", 12, 18), [[1, 6]], 6, 0)
+    send(0)
+    iota(v("byh"), [[0, 4], [APART - 1, 2], [0, 64]], 1, 0)
+    sel(v("kt", 512, 1024), v("byh"), [[0, 8], [-1, 16], [0, 4]], A.is_equal, 0.0, 0, 1)
+    sel(v("sm", 512, 640), v("cin", 256, 384), [[1, 128]], A.is_ge, 0.0, 0, -1)
+    iota(v("c32"), [[1, 12]], 0, 0)
     iota(v("kv"), [[16, 6], [96, 2], [1, 16]], 0, 0)
-    iota(v("wh", 0, 416), [[1, 416]], K, 0)
-    iota(v("wh", 416, 1248), [[0, 2], [1, 416]], K, 0)
+    iota(v("wh", 0, 1024), [[0, 2], [1, 512]], K, 0)
     send(1)
+    iota(v("wh", 1024, 2048), [[0, 2], [1, 512]], K, 0)
     send(2)
 
     cp(v("pu"), v("p32"))
@@ -240,7 +255,7 @@ def build(T, topo, core):
     ts(c1("pi", 3), c1("p32", 0), 4, A.logical_shift_right, 1, A.bitwise_and)
     ts(c1("pi", 4), c1("p32", 0), 4, A.logical_shift_right)
     cp(v("col", 0, 5), v("pi", 0, 5))
-    q_, h_, g_, wt_, r2_, r2b_, hq_, nh_, junk_, junk2_ = [c1("col", j) for j in range(2, 12)]
+    q_, h_, g_, bit_, tiny_, not2_, is2_, hq_, nh_, junk_, junk2_, s1_, s2_, end_ = [c1("col", j) for j in range(2, 16)]
     cp(v("pku", 0, 8), v("pk32", 0, 8))
     ts(v("pkf"), v("pk32", 8, 16), c1("col", 0), A.add, c1("col", 1), A.add)
     ts(v("pku", 8, 16), v("pkf"), 1.0, A.add)
@@ -248,52 +263,60 @@ def build(T, topo, core):
     act(v("khold"), ind(v("sm", 128, 256), v("pu")), F.Copy)
     for i in range(6):
         ms(v("ct", 4 * (TOFF[i] + 16 * SLOTS[i][3]), 4 * (TOFF[i] + TILES[i])), 0.0)
-    ms(c1("rs", 0), 0.0)
+    for j in range(2):
+        quant(v("qr", 128 * j, 128 * j + 128), v("sr", 128 * j, 128 * j + 128), v("kr", 2 - 2 * j, 514 - 2 * j))
     ms(v("pw", 0, 16), 0.0)
     ms(v("yt", 384, 544), 0.0)
-    ms(v("rw", 0, 16), 0.0)
-    ms(v("rw", 0, 14, 13), 1.0)
-    ms(v("rw", 1, 13, 11), 16.0)
-    ms(v("rw", 5, 9, 3), 256.0)
-    ms(v("rw", 4, 10, 5), 4096.0)
+    ms(v("rw", 0, 32), 0.0)
+    for a, b, w in ((0, 13, 0.5), (1, 12, 8.0), (8, 5, 128.0), (9, 4, 2048.0)):
+        aff(v("rw", a, a + 17, 16), v("rw", a, a + 17, 16), 1.0, w)
+        aff(v("rw", b, b + 17, 16), v("rw", b, b + 17, 16), 1.0, w / 4096 / APART)
+    aff(v("rw", 6, 15, 8), v("rw", 6, 15, 8), 1.0, 1024.0)
+    aff(v("rw", 7, 31, 23), v("rw", 7, 31, 23), 1.0, float(K))
     quant(v("qu"), v("su"), v("ut"))
     for j in range(2):
         cp(v("qu2", 128 * j, 128 * j + 128), ind(v("qu"), v("pku", 8 * j, 8 * j + 8)), dt.uint32)
         act(v("su2", 128 * j, 128 * j + 128), ind(v("su"), v("pku", 8 * j, 8 * j + 8)), F.Copy)
     quant(v("qx", 0, 192), v("sx", 0, 192), v("xt", 0, 768))
     quant(v("qx", 192, 384), v("sx", 192, 384), v("xt", 768, 1536))
-    tt(v("rw", 16, 32), v("rw", 0, 16), v("cmin", 0, 16), A.min)
-    add("v", lambda e: e.tensor_reduce(ap(wt_), ap(v("rw", 16, 32)), AxisListType.X, A.max), [v("rw", 16, 32)], [wt_], 64)
+    tt(v("rw", 32, 64), v("rw", 0, 32), v("cmin", 0, 32), A.min)
+    scan(v("rw", 64, 96), v("khold", 0, 32), v("rw", 32, 64), -BIG, A.min, A.max)
+    top_, foot_ = c1("rw", 79), c1("rw", 95)
+    ts(v("stair"), v("iot"), top_, A.min, foot_, A.max)
+    tt(bit_, top_, foot_, A.is_equal)
+    ts(tiny_, bit_, 0.0, A.is_equal, -TINY, A.add)
     ts(v("kt", 0, 512), v("grp"), g_, A.is_equal)
     quant(v("qk", 0, 128), v("sk", 0, 128), v("kt", 0, 512))
     cp(v("lu"), v("l32"))
     cp(v("mu"), v("m32"))
-    ts(r2_, q_, 2.0, A.is_equal)
-    ts(r2b_, q_, 2.0, A.is_equal, -192.0, A.mult)
-    act(v("lm"), ind(v("iot"), v("lu")), F.Identity, bias=r2b_, scale=r2_)
-    act(v("lmb"), ind(v("iot"), v("mu")), F.Identity, bias=-192.0)
-    dma("y", lambda: T.lm[10:128:16, :], lambda: T.lmb[10:128:16, :], [v("lmb")], [v("lm")])
-    act(v("cxw"), ind(v("sm", 384, 512), v("pu")), F.Copy)
-    ts(v("cxw", 15, C, 16), v("cxw", 15, C, 16), -4096.0, A.add)
-    dma("y", lambda: T.cxr[:], lambda: T.cxw[:], [v("cxw")], [v("cxr")])
+    ts(not2_, q_, 6.0, A.not_equal)
+    aff(is2_, not2_, -float(K), float(K))
+    act(v("cxr"), ind(v("sm", 384, 512), v("pu")), F.Copy)
+    aff(end_, c1("cxr", 15), 1.0, -4096.0)
     ts(hq_, h_, 16.0, A.mult, q_, A.subtract)
-    ts(v("base"), v("base"), hq_, A.add)
-    tt(v("base"), v("base"), v("cxw", 15, C, 16), A.add)
-    ts(nh_, h_, -1.0, A.mult, 1.0, A.add)
-    ts(junk_, q_, 384.0, A.add)
-    ts(junk2_, q_, 400.0, A.add)
+    aff(hq_, hq_, 1.0, end_)
+    aff(v("base"), v("base"), 1.0, hq_)
+    aff(v("base", 1, 2 * NPAIR, 2), v("base", 1, 2 * NPAIR, 2), 1.0, ROUND / 512)
+    aff(v("base", 2, 17, 2), v("base", 2, 17, 2), 1.0, -128.0)
+    for c in range(18, 2 * NPAIR + 1, 2):
+        aff(c1("base", c), c1("base", c), 1.0, -8.0 * c)
+    aff(nh_, h_, -float(APART), float(APART))
+    aff(junk_, q_, 1.0, 384.0)
+    aff(junk2_, q_, 1.0, 400.0)
     quant(v("qk", 128, 256), v("sk", 128, 256), v("kt", 512, 1024))
     ms(v("kb"), 1.0)
-    ms(v("kb", 0, 48, 4), 0.0)
-    ts(v("kb", 2, 48, 4), v("kb", 1, 48, 4), nh_, A.mult, 65536.0, A.mult)
-    ts(v("m48"), v("m48"), h_, A.is_equal)
+    aff(v("kb", 0, 48, 4), v("kb", 0, 48, 4), 0.0, 0.0)
+    aff(v("kb", 2, 48, 4), v("kb", 2, 48, 4), nh_, 0.0)
+    aff(s1_, h_, -2048.0, 1024.0)
+    aff(s2_, h_, 1024.0, -1536.0)
+    aff(v("pk", 0, 24, 2), v("kb", 1, 48, 4), s1_, 0.0)
+    aff(v("pk", 1, 24, 2), v("kb", 1, 48, 4), s2_, 0.0)
     for b in range(4):
         quant(v("qe", 128 * b, 128 * b + 128), v("se", 128 * b, 128 * b + 128), v("et", 3 - b, 515 - b))
-    ms(v("camp", K, 288), 1.0)
-    ms(v("camp", K + 15, 288, 16), 2.0 ** -6)
-    act(v("camp", 0, K), ind(v("sm", 512, 640), v("pu", 0, 12)), F.Copy)
+    ms(v("eq", 0, K, 2), 0.0)
+    act(v("camp", 0, C, 2), ind(v("sm", 512, 640), v("pu", 0, 12)), F.Copy)
+    act(v("camp", 1, C, 2), ind(v("sm", 512, 640), v("pu", 0, 12)), F.Identity, scale=-1.0)
     cp(v("repu"), v("c32"))
-    ms(v("camp", 15, K, 16), 2.0 ** -12)
     quant(v("qv"), v("sv"), v("vt"))
 
     def slot(c):
@@ -317,34 +340,54 @@ def build(T, topo, core):
         mm(bank(0, C), ub[0], ub[1], v("qx"), v("sx"))
         mm(bank(2, C), v("qu2", 128, 256), v("su2", 128, 256), v("qx"), v("sx"))
         mm(bank(1, C), ub[0], ub[1], v("qx"), v("sx"))
-        for b in range(4):
-            mm(bank(4 + b, C), eq_(b)[0], eq_(b)[1], v("qx"), v("sx"))
-            act(v("tv", 576 * b + K, 576 * b + 576), bank(4 + b, C), F.Copy)
-        tt(v("m1"), bank(0, C), v("cmin"), A.min)
-        scan(v("hh"), v("khold"), v("m1"), -BIG, A.min, A.max)
-        act(v("sgb"), bank(2, C), F.Sign)
-        act(v("bw"), v("sgb"), F.Relu, scale=wt_)
-        tt(v("x1"), ind(v("bw"), v("mu")), v("lm"), A.subtract)
-        tt(v("pay"), ind(v("bw"), v("lu")), v("x1"), A.subtract)
+        for a, b in ((K, C), (0, K)):
+            tt(v("m1", a, b), bank(0, b, a), v("cmin", a, b), A.min)
+            scan(v("hh", a, b), v("khold", a, b), v("m1", a, b), -BIG, A.min, A.max)
+        act(v("sgb"), bank(2, C), F.Sign, bias=tiny_, scale=bit_)
+        scan(v("bw"), v("stair"), v("sgb"), 0.0, A.max, A.mult)
+        act(v("x1"), ind(v("bw"), v("lu")), F.Identity, bias=is2_, scale=not2_)
+        tt(v("pay"), ind(v("bw"), v("mu")), v("x1"), A.subtract)
         tt(slot(0), bank(0, C), v("hh"), A.is_le)
         scan(v("rd"), v("keep"), slot(0), 0.0, A.min, A.add)
-        tt(v("base2"), v("base"), v("rd", 15, C, 16), A.subtract)
+        tt(v("cxr", 15, C, 16), v("base"), v("rd", 15, C, 16), A.subtract)
         for c in range(23, 0, -1):
             z = c1("hh", 16 * c + 15)
-            if c in S_ROWS:
+            if c > 2 * NPAIR:
                 s = v("sg", ROFF[c], ROFF[c + 1])
                 act(s, bank(1, 16 * c), F.Sign, bias=z, scale=-1.0)
                 act(slot(c), s, F.Relu, acc=c1("rs", c))
             else:
                 ts(slot(c), bank(0, 16 * c), z, A.is_lt)
-                act(v("jk", ROFF[c], ROFF[c + 1]), slot(c), F.Identity, acc=c1("rs", c))
-        for i in range(6):
+        for i in (2, 3, 4, 5, 1, 0):
             a, w = TOFF[i], TILES[i]
-            quant(v("qc", a, a + w), v("sc", a, a + w), v("ct", 4 * a, 4 * (a + w)))
-            mm(bank(3, w), kq(0)[0], kq(0)[1], v("qc", a, a + w), v("sc", a, a + w), i == 0, i == 5)
-        tt(v("cxr", 15, C, 16), v("base2"), v("rs"), A.subtract)
+            if i != 5:
+                wq = 256 if i == 4 else w
+                quant(v("qc", a, a + wq), v("sc", a, a + wq), v("ct", 4 * a, 4 * (a + wq)))
+            if i == 2:
+                w = C
+            mm(bank(3, w), kq(0)[0], kq(0)[1], v("qc", a, a + w), v("sc", a, a + w), i == 2, i == 0)
+            for bk, (ti, hf, a0, nw, calls, outs) in zip(SUMBANK, SUMS):
+                if ti == i and outs[0][0] < NPAIR:
+                    for j in range(calls):
+                        x = a + a0 + nw * j
+                        mm(bank(bk, nw), v("qr", 128 * hf, 128 * hf + 128), v("sr", 128 * hf, 128 * hf + 128),
+                           v("qc", x, x + nw), v("sc", x, x + nw), j == 0, j == calls - 1)
+                    for pr, x, nc in outs:
+                        act(v("jk", 160 * pr, 160 * pr + nc), bank(bk, x + nc, x), F.Identity, bias=-max(1.0, 128.0 / nc), acc=c1("pp", pr))
+        for b in range(4):
+            mm(bank(4 + b, C), eq_(b)[0], eq_(b)[1], v("qx"), v("sx"))
+            act(v("tv", 576 * b + K, 576 * b + 576), bank(4 + b, C), F.Copy)
+        odd, even = v("cxr", 31, 32 * NPAIR, 32), v("cxr", 47, 32 * NPAIR + 16, 32)
+        rest = v("cxr", 32 * NPAIR + 31, C, 16)
+        ts(v("ph", 0, NPAIR), v("pp", 0, NPAIR), ROUND, A.add, ROUND, A.subtract)
+        act(v("ph2", 0, NPAIR), v("pp", 0, NPAIR), F.Identity, bias=ROUND / 512, scale=1.0 / 512)
+        tt(even, even, v("pp", 0, NPAIR), A.subtract)
+        tt(even, even, v("ph", 0, NPAIR), A.add)
+        tt(odd, odd, v("ph2", 0, NPAIR), A.subtract)
+        tt(rest, rest, v("rs", 2 * NPAIR + 1, 24), A.subtract)
         scan(v("xs"), bank(3, C), v("cxr"), -1.0, A.max, A.add)
         ts(v("rk"), v("xs", 15, C, 16), 3072.0, A.add)
+        aff(v("cxr", 15, C, 16), v("base"), 0.0, end_)
         cp(ind(v("pw"), v("rk")), v("pay"))
         turn(v("yt", 0, 192), v("pw", 0, 192))
         turn(v("yt", 192, 384), v("pw", 16, 208))
@@ -353,19 +396,20 @@ def build(T, topo, core):
         scan(v("b48"), v("kb"), v("w1"), 0.0, A.mult, A.add)
         for j in range(2):
             mm(bank(0, 128), kq(1)[0], kq(1)[1], ym(2 * j)[0], ym(2 * j)[1], j == 0, j == 1)
-        tt(v("w48"), v("yt", 2, 384, 8), v("m48"), A.mult)
-        tt(v("ab", 0, 12), v("w48", 0, 48, 4), v("w48", 2, 48, 4), A.add)
-        tt(v("ab", 12, 24), v("w48", 1, 48, 4), v("w48", 3, 48, 4), A.add)
-        ts(v("ab2"), v("ab"), 192.0, A.add)
-        tt(v("ee"), v("ab", 12, 24), v("ab", 0, 12), A.subtract)
+        scan(v("pko", 0, 24), v("yt", 6, 384, 16), v("pk"), -512.0, A.max, A.add)
+        scan(v("pko", 24, 48), v("yt", 7, 384, 16), v("pk"), -512.0, A.max, A.add)
+        scan(v("pko", 48, 72), v("yt", 14, 384, 16), v("pk"), 512.0, A.min, A.subtract)
+        ts(v("ab2", 12, 24), v("pko", 1, 24, 2), 512.0 + K, A.add)
+        tt(v("ee"), v("pko", 25, 48, 2), v("pko", 49, 72, 2), A.add)
+        tt(v("ab2", 0, 12), v("ab2", 12, 24), v("ee"), A.subtract)
         tt(v("ppi"), bank(0, 96, 0, 8), v("b48", 3, 48, 4), A.mult)
         ts(v("fl"), v("ppi"), 3, A.arith_shift_right, 1, A.bitwise_and)
         tt(v("fe"), v("fl"), v("ee"), A.mult)
         tt(v("lr", 0, 12), v("ab2", 0, 12), v("fe"), A.add)
         tt(v("lr", 12, 24), v("ab2", 12, 24), v("fe"), A.subtract)
         cp(v("lru"), v("lr"))
-        act(v("ff", 0, K), ind(v("iot"), v("lru", 0, 12)), F.Copy)
-        act(v("ff", K, 288), ind(v("iot"), v("lru", 0, 6)), F.Copy)
+        act(v("ff"), ind(v("lr", 0, 12), v("repu")), F.Copy)
+        act(v("camp", 31, C, 32), v("lr", 0, 12), F.Identity, bias=-3.0, scale=-1.0 / 512)
         for b in range(4):
             tw = v("tv", 576 * b + K, 576 * b + 576)
             act(v("ln", K * b, K * b + K), ind(tw, v("lru", 0, 12)), F.Copy)
@@ -374,32 +418,29 @@ def build(T, topo, core):
         arrived(t)
         for b in range(4):
             mm(bank(4 + b, K), v("wq%d" % t, 128 * b, 128 * b + 128), v("wp%d" % t, 128 * b, 128 * b + 128), v("qm"), v("smm"))
-            act(v("ht", b, 4 * K, 4), bank(4 + b, K), F.Identity, scale=0.03125)
+            if b in HT_V:
+                ts(v("ht", b, 4 * K, 4), bank(4 + b, K), 0.03125, A.mult)
+            else:
+                act(v("ht", b, 4 * K, 4), bank(4 + b, K), F.Identity, scale=0.03125)
         quant(v("qh"), v("sh"), v("ht"))
         for b in range(4):
             mm(bank(b, K), eq_(b)[0], eq_(b)[1], v("qh"), v("sh"))
             tt(v("tv", 576 * b, 576 * b + K), bank(b, K), v("ln", K * b, K * b + K), A.add)
-        tt(v("eq"), ind(v("lr", 0, 12), v("repu")), v("ff"), A.is_equal)
-        scan(v("es"), v("eq"), v("camp"), 0.0, A.add, A.mult)
-        tt(v("es", 111, K, 16), v("es", 111, K, 16), v("es", K + 15, 288, 16), A.max)
-        ts(v("d1", 0, 6), v("es", 15, 96, 16), 48.0 / 4096.0, A.is_gt, junk_, A.mult)
-        ts(v("d1", 6, 12), v("es", 111, K, 16), 48.0 / 4096.0, A.is_gt, junk2_, A.mult)
-        tt(v("d2"), v("d1"), v("lr", 0, 12), A.max)
-        cp(v("du", 0, 12, 2), v("d2", 0, 6))
-        cp(v("du", 1, 12, 2), v("d2", 6, 12))
+        tt(v("eq", 1, C, 2), ind(v("iot"), v("lru", 0, 12)), v("ff"), A.is_equal)
+        tt(v("eq", K, C, 2), ind(v("iot"), v("lru", 0, 6)), v("ff", 96, K), A.is_equal)
+        scan(v("es"), v("eq"), v("camp"), 0.0, A.max, A.add)
+        ts(v("du", 0, 12, 2), v("es", 31, K, 32), -512.0, A.mult, junk_, A.max)
+        ts(v("du", 1, 12, 2), v("es", K + 31, C, 32), -512.0, A.mult, junk2_, A.max)
         for c in range(5, -1, -1):
-            cp(ind(v("wh", 416 * t, 416 * t + 416), v("du", 2 * c, 2 * c + 2)), v("kv", 32 * c, 32 * c + 32))
-        scan(v("xw"), v("wh", 416 * t, 416 * t + C), v("cxw"), -1.0, A.max, A.add)
+            cp(ind(v("wh", 512 * t, 512 * t + 896), v("du", 2 * c, 2 * c + 2)), v("kv", 32 * c, 32 * c + 32))
+        scan(v("xw"), v("wh", 512 * t + 512, 512 * t + 896), v("cxr"), -1.0, A.max, A.add)
         ts(v("wu"), v("xw", 15, C, 16), 3072.0, A.add)
         for b in range(4):
-            w = v("tv", 576 * b, 576 * b + 576)
-            if b < 2:
-                act(v("xt", b, 4 * C, 4), ind(w, v("wu")), F.Identity, scale=-2.0)
-            elif b == 3:
-                ts(v("xt", b, 4 * C, 4), ind(w, v("wu")), -2.0, A.mult)
-            else:
-                act(v("xt", b, 2 * C, 4), ind(w, v("wu", 0, 12)), F.Identity, scale=-2.0)
-                ts(v("xt", 2 * C + b, 4 * C, 4), ind(w, v("wu", 12, 24)), -2.0, A.mult)
+            w, x = v("tv", 576 * b, 576 * b + 576), XT_S[b]
+            if x:
+                act(v("xt", b, 64 * x, 4), ind(w, v("wu", 0, x)), F.Identity, scale=-2.0)
+            if x < 24:
+                ts(v("xt", 64 * x + b, 4 * C, 4), ind(w, v("wu", x, 24)), -2.0, A.mult)
         if t < R - 1:
             quant(v("qx"), v("sx"), v("xt"))
 
@@ -464,9 +505,11 @@ def plan(ops):
         tail[i] = ns[i] + max([0.0] + [lag[k][i] + tail[k] for k in after[i]])
     pre = [[(j, ns[j] + lag[i][j]) for j in deps[i]] for i in range(n)]
 
-    def lay(key):
-        busy, start, left = dict((q, []) for q in "vspgy"), [0.0] * n, [len(d) for d in deps]
-        ready = sorted((key[i], i) for i in range(n) if not left[i])
+    def lay(key, lo, hi, busy, start):
+        busy, start = dict((q, list(b)) for q, b in busy.items()), list(start)
+        left = [0] * lo + [sum(1 for j in deps[i] if j >= lo) for i in range(lo, hi)] if (lo, hi) not in lefts else list(lefts[lo, hi])
+        lefts.setdefault((lo, hi), list(left))
+        ready = sorted((key[i], i) for i in range(lo, hi) if not left[i])
         while ready:
             i = ready.pop(0)[1]
             s = 0.0
@@ -484,23 +527,42 @@ def plan(ops):
             start[i] = s
             new = False
             for k in after[i]:
-                left[k] -= 1
-                if not left[k]:
-                    ready.append((key[k], k))
-                    new = True
+                if k < hi:
+                    left[k] -= 1
+                    if not left[k]:
+                        ready.append((key[k], k))
+                        new = True
             if new:
                 ready.sort()
-        return max(start[i] + ns[i] for i in range(n)), start
+        return max(start[i] + ns[i] for i in range(lo, hi) if qs[i] != "g"), start, busy
 
-    best = lay([-x for x in tail])
-    rng = np.random.RandomState(1)
-    for _ in range(PASSES):
-        mid, wide, sd = rng.uniform(0, best[0]), rng.uniform(500, 3000), rng.choice([300.0, 1000.0, 3000.0])
-        k2 = [best[1][i] + (sd * float(rng.randn()) if abs(best[1][i] - mid) < wide and rng.rand() < 0.15 else 0.0) for i in range(n)]
-        got = lay(k2)
-        if got[0] <= best[0]:
-            best = got
-    return sorted(range(n), key=lambda k: (best[1][k], k))
+    lefts, rng = {}, np.random.RandomState(1)
+    cuts = [0] + [i + 1 for i in range(n) if ops[i][3][:1] == [v("qx")]] + [n]
+
+    def vary(key, lo, hi, busy, start, t0, passes):
+        best = now = lay(key, lo, hi, busy, start)
+        for step in range(passes):
+            mid, wide = t0 + float(rng.rand()) * (now[0] - t0), 300 + 2500 * float(rng.rand())
+            at = np.array(now[1])
+            move = (np.abs(at - mid) < wide) & (rng.rand(n) < 0.15)
+            got = lay((at + move * rng.randn(n) * (200.0, 600.0, 2000.0)[step % 3]).tolist(), lo, hi, busy, start)
+            if got[0] <= now[0] + 100.0 * float(rng.rand()) * (1.0 - step / passes) ** 2:
+                now = got
+                if now[0] < best[0]:
+                    best = now
+        return best
+
+    busy, per = dict((q, []) for q in "vspgy"), cuts[2] - cuts[1]
+    one = vary([-x for x in tail], cuts[1], cuts[2], busy, [-1e5] * n, 0.0, 2 * PASSES)[1][cuts[1]:cuts[2]]
+    start, t0 = [0.0] * n, 0.0
+    for lo, hi in zip(cuts, cuts[1:]):
+        a = hi - per if lo == 0 else lo
+        key = [1e9] * n
+        key[a:a + per] = [x + (t0 or 4000.0) for x in one]
+        for i in range(a - 1, lo - 1, -1):
+            key[i] = min([1e9] + [key[k] - ns[i] - lag[k][i] for k in after[i] if k < hi])
+        t0, start, busy = vary(key, lo, hi, busy, start, t0, 2 * PASSES if lo == 0 else PASSES // 2)
+    return sorted(range(n), key=lambda k: (start[k], k))
 
 
 def order(ops):

@@ -10,19 +10,22 @@ WIDE = {BF: 2, F32: 4, I32: 4, U16: 2, Q4: 4, U8: 1}
 TILES = [384, 320, 256, 192, 128, 128]
 SLOTS = [[0, 23, 22, 21], [20, 19, 18, 17], [16, 15, 14, 13], [12, 11, 10, 9], [8, 7, 6, 5], [4, 3, 2, 1]]
 TOFF = [0, 384, 704, 1088, 1280, 1408]
-NPAIR = 9
+NPAIR = 10
 SUMS = [(2, 0, 0, 128, 2, [(7, 0, 128)]), (2, 1, 0, 128, 2, [(6, 0, 128)]), (3, 0, -64, 128, 2, [(5, 0, 128)]),
-        (3, 1, -64, 128, 2, [(4, 0, 128)]), (4, 0, 0, 256, 1, [(3, 0, 128), (1, 128, 64)]),
-        (4, 1, 0, 256, 1, [(2, 0, 128), (0, 128, 32)]), (1, 1, 0, 144, 2, [(8, 0, 144)]), (1, 0, 0, 160, 2, [(9, 0, 160)])]
-SUMBANK = [4, 5, 6, 7, 2, 4, 5, 6]
+        (3, 1, -64, 128, 2, [(4, 0, 128)]), (4, 0, 0, 128, 1, [(3, 0, 128)]), (4, 1, 0, 128, 1, [(2, 0, 128)]),
+        (1, 1, 0, 144, 2, [(8, 0, 144)]), (1, 0, 0, 160, 2, [(9, 0, 160)]), (5, 0, 0, 128, 1, [(1, 0, 64)]),
+        (5, 1, 0, 128, 1, [(0, 0, 32)]), (0, 1, 0, 128, 3, [(10, 0, 128)])]
+SUMBANK = [5, 6, 7, 4, 2, 5, 6, 7, 4, 2, 4]
+PAIR0, S_ROWS, TORDER = 2, (23, 22, 21, 4, 3, 2, 1), (2, 3, 4, 1, 0, 5)
 ROUND = 1.5 * 2.0 ** 32
-XT_S = (24, 24, 6, 0)
+XT_V = {(12, 2): 12, (12, 3): 12, (0, 3): 12, (0, 2): 4}
+BY_SCAN = True
 HT_V = (1, 3)
 APART = 32768
 TINY = 2.0 ** -110
 ROFF = [8 * c * (c - 1) for c in range(25)]
 CY, PE, GAT, SCA, WAKE = 0.85, 0.6, 1.5, 3.5, 180.0
-PASSES = 8000
+PASSES = 12000
 
 
 def _sb(n, d):
@@ -36,12 +39,12 @@ SCRATCH = {
     "wq": _sb(512, Q4), "wp": _sb(512, U8),
     "wq0": _sb(512, Q4), "wp0": _sb(512, U8), "wq1": _sb(512, Q4), "wp1": _sb(512, U8), "wq2": _sb(512, Q4), "wp2": _sb(512, U8),
     "l32": _sb(24, I32), "m32": _sb(24, I32), "lu": _sb(24, U16), "mu": _sb(24, U16),
-    "half": _sb(516, BF), "et": _sb(516, BF), "qe": _sb(512, Q4), "se": _sb(512, U8),
+    "et": _sb(520, BF), "qe": _sb(512, Q4), "se": _sb(512, U8),
     "grp": _sb(512, BF), "byh": _sb(512, BF), "kt": _sb(1024, BF), "qk": _sb(256, Q4), "sk": _sb(256, U8),
     "kb": _sb(48, F32), "w1": _sb(48, F32), "b48": _sb(48, F32),
     "ct": _sb(4 * 1536, BF), "qc": _sb(1536, Q4), "sc": _sb(1536, U8),
-    "jk": _sb(1600, F32), "sg": _sb(4416, BF), "two": _sb(516, BF), "kr": _sb(516, BF), "qr": _sb(256, Q4), "sr": _sb(256, U8),
-    "pp": _sb(10, F32), "ph": _sb(10, F32), "ph2": _sb(10, F32),
+    "jk": _sb(1760, F32), "sg": _sb(4416, BF), "two": _sb(2 * C, BF), "kr": _sb(516, BF), "qr": _sb(256, Q4), "sr": _sb(256, U8),
+    "ph": _sb(24, F32),
     "cin": _sb(3 * 128, F32), "sm": _sb(5 * 128, F32),
     "p32": _sb(24, I32), "pu": _sb(24, U16), "c32": _sb(12, I32), "repu": _sb(12, U16),
     "pi": _sb(8, I32), "col": _sb(16, F32), "pk32": _sb(16, I32), "pkf": _sb(8, F32), "pku": _sb(16, U16),
@@ -53,7 +56,7 @@ SCRATCH = {
     "yt": _sb(544, BF), "qy": _sb(136, Q4), "sy": _sb(136, U8),
     "ab2": _sb(24, F32), "ee": _sb(12, F32),
     "ppi": _sb(12, I32), "fl": _sb(12, I32), "fe": _sb(12, F32), "lr": _sb(24, F32), "lru": _sb(24, U16),
-    "tv": _sb(4 * 576, BF), "ln": _sb(4 * K, BF), "mt": _sb(4 * K, BF), "qm": _sb(K, Q4), "smm": _sb(K, U8),
+    "tv": _sb(4 * 576, BF), "ln": _sb(4 * C, BF), "mt": _sb(4 * K, BF), "qm": _sb(K, Q4), "smm": _sb(K, U8),
     "ht": _sb(4 * K, BF), "qh": _sb(K, Q4), "sh": _sb(K, U8),
     "ff": _sb(K, F32), "eq": _sb(C, F32), "es": _sb(C, F32), "du": _sb(12, U16),
     "xw": _sb(C, F32), "wu": _sb(24, U16), "olu": _sb(24, U16), "olf": _sb(C, F32), "yf": _sb(C, F32),
@@ -219,24 +222,23 @@ def build(T, topo, core):
     ms(v("cin", 0, 128), BIG)
     ms(v("two"), 0.0)
     quant(v("qc", 960, 1088), v("sc", 960, 1088), v("two", 0, 512))
-    aff(v("half"), v("two"), 1.0, -0.5)
-    aff(v("two", 2, 516, 4), v("two", 2, 516, 4), 1.0, 1.0)
+    aff(v("two", 2, 2 * C, 4), v("two", 2, 2 * C, 4), 1.0, 1.0)
     aff(v("two", 3, 516, 4), v("two", 3, 516, 4), 1.0, 512.0)
-    aff(v("cin", 128, 256), v("cin", 0, 128), 0.0, 1024.0)
-    aff(v("cin", 256, 384), v("cin", 0, 128), 0.0, 2.0)
     iota(v("p32"), [[0, 24]], 0, 1)
     sel(v("sm", 0, 128), v("cin", 0, 128), [[1, 128]], A.is_equal, -BIG, 0, -1)
     sel(v("sm", 128, 256), v("cin", 0, 128), [[1, 128]], A.is_gt, -BIG, 0, -1)
     iota(v("pk32"), [[0, 2], [16, 8]], 0, 0)
     iota(v("grp"), [[1, 8], [0, 64]], 0, 0)
-    sel(v("kr"), v("two"), [[-1, 129], [0, 4]], A.is_equal, 0.0, 0, 1)
+    sel(v("kr"), v("two", 0, 516), [[-1, 129], [0, 4]], A.is_equal, 0.0, 0, 1)
+    aff(v("two", 1, 520, 4), v("two", 1, 520, 4), 1.0, -0.5)
     iota(v("iot"), [[1, C]], 0, 0)
+    iota(v("cin", 128, 384), [[-1022, 2], [0, 128]], 1024, 0)
     sel(v("sm", 256, 384), v("cin", 128, 256), [[1, 128]], A.is_equal, 0.0, 0, -1)
-    iota(v("base"), [[16, 24]], 15, 0)
+    iota(v("base"), [[16, 24]], 3072 + 15, 0)
     sel(v("sm", 384, 512), v("sm", 256, 384), [[1, 128]], A.is_ge, -4096.0, 0, -1)
     ms(v("keep"), 64.0)
     ms(v("keep", 0, C, 16), 0.0)
-    sel(v("et"), v("half"), [[-1, 516]], A.is_equal, 0.0, 3, 4)
+    sel(v("et"), v("two", 0, 520), [[-1, 520]], A.is_equal, 0.0, 5, 4)
     send(0)
     iota(v("byh"), [[0, 4], [APART - 1, 2], [0, 64]], 1, 0)
     sel(v("kt", 512, 1024), v("byh"), [[0, 8], [-1, 16], [0, 4]], A.is_equal, 0.0, 0, 1)
@@ -255,7 +257,7 @@ def build(T, topo, core):
     ts(c1("pi", 3), c1("p32", 0), 4, A.logical_shift_right, 1, A.bitwise_and)
     ts(c1("pi", 4), c1("p32", 0), 4, A.logical_shift_right)
     cp(v("col", 0, 5), v("pi", 0, 5))
-    q_, h_, g_, bit_, tiny_, not2_, is2_, hq_, nh_, junk_, junk2_, s1_, s2_, end_ = [c1("col", j) for j in range(2, 16)]
+    q_, h_, g_, bit_, tiny_, not6_, is6_, hq_, nh_, junk_, junk2_, s1_, s2_ = [c1("col", j) for j in range(2, 15)]
     cp(v("pku", 0, 8), v("pk32", 0, 8))
     ts(v("pkf"), v("pk32", 8, 16), c1("col", 0), A.add, c1("col", 1), A.add)
     ts(v("pku", 8, 16), v("pkf"), 1.0, A.add)
@@ -265,6 +267,8 @@ def build(T, topo, core):
         ms(v("ct", 4 * (TOFF[i] + 16 * SLOTS[i][3]), 4 * (TOFF[i] + TILES[i])), 0.0)
     for j in range(2):
         quant(v("qr", 128 * j, 128 * j + 128), v("sr", 128 * j, 128 * j + 128), v("kr", 2 - 2 * j, 514 - 2 * j))
+    ms(v("rs"), 0.0)
+    aff(v("ph"), v("rs"), 1.0, 0.0)
     ms(v("pw", 0, 16), 0.0)
     ms(v("yt", 384, 544), 0.0)
     ms(v("rw", 0, 32), 0.0)
@@ -277,8 +281,6 @@ def build(T, topo, core):
     for j in range(2):
         cp(v("qu2", 128 * j, 128 * j + 128), ind(v("qu"), v("pku", 8 * j, 8 * j + 8)), dt.uint32)
         act(v("su2", 128 * j, 128 * j + 128), ind(v("su"), v("pku", 8 * j, 8 * j + 8)), F.Copy)
-    quant(v("qx", 0, 192), v("sx", 0, 192), v("xt", 0, 768))
-    quant(v("qx", 192, 384), v("sx", 192, 384), v("xt", 768, 1536))
     tt(v("rw", 32, 64), v("rw", 0, 32), v("cmin", 0, 32), A.min)
     scan(v("rw", 64, 96), v("khold", 0, 32), v("rw", 32, 64), -BIG, A.min, A.max)
     top_, foot_ = c1("rw", 79), c1("rw", 95)
@@ -289,17 +291,16 @@ def build(T, topo, core):
     quant(v("qk", 0, 128), v("sk", 0, 128), v("kt", 0, 512))
     cp(v("lu"), v("l32"))
     cp(v("mu"), v("m32"))
-    ts(not2_, q_, 6.0, A.not_equal)
-    aff(is2_, not2_, -float(K), float(K))
+    ts(not6_, q_, 6.0, A.not_equal)
+    aff(is6_, not6_, -float(K), float(K))
     act(v("cxr"), ind(v("sm", 384, 512), v("pu")), F.Copy)
-    aff(end_, c1("cxr", 15), 1.0, -4096.0)
+    aff(v("cxr", 15, C, 16), v("cxr", 15, C, 16), 1.0, -4096.0)
     ts(hq_, h_, 16.0, A.mult, q_, A.subtract)
-    aff(hq_, hq_, 1.0, end_)
     aff(v("base"), v("base"), 1.0, hq_)
-    aff(v("base", 1, 2 * NPAIR, 2), v("base", 1, 2 * NPAIR, 2), 1.0, ROUND / 512)
-    aff(v("base", 2, 17, 2), v("base", 2, 17, 2), 1.0, -128.0)
-    for c in range(18, 2 * NPAIR + 1, 2):
-        aff(c1("base", c), c1("base", c), 1.0, -8.0 * c)
+    aff(v("base", 2 * PAIR0 + 1, 2 * NPAIR, 2), v("base", 2 * PAIR0 + 1, 2 * NPAIR, 2), 1.0, ROUND / 512)
+    aff(v("base", 2 * PAIR0 + 2, 2 * NPAIR + 1, 2), v("base", 2 * PAIR0 + 2, 2 * NPAIR + 1, 2), 1.0, -128.0)
+    for c in (18, 20):
+        aff(c1("base", c), c1("base", c), 1.0, 128.0 - 8.0 * c)
     aff(nh_, h_, -float(APART), float(APART))
     aff(junk_, q_, 1.0, 384.0)
     aff(junk2_, q_, 1.0, 400.0)
@@ -312,7 +313,7 @@ def build(T, topo, core):
     aff(v("pk", 0, 24, 2), v("kb", 1, 48, 4), s1_, 0.0)
     aff(v("pk", 1, 24, 2), v("kb", 1, 48, 4), s2_, 0.0)
     for b in range(4):
-        quant(v("qe", 128 * b, 128 * b + 128), v("se", 128 * b, 128 * b + 128), v("et", 3 - b, 515 - b))
+        quant(v("qe", 128 * b, 128 * b + 128), v("se", 128 * b, 128 * b + 128), v("et", 5 - b, 517 - b))
     ms(v("eq", 0, K, 2), 0.0)
     act(v("camp", 0, C, 2), ind(v("sm", 512, 640), v("pu", 0, 12)), F.Copy)
     act(v("camp", 1, C, 2), ind(v("sm", 512, 640), v("pu", 0, 12)), F.Identity, scale=-1.0)
@@ -335,59 +336,68 @@ def build(T, topo, core):
     def ym(s):
         return v("qy", s, s + 128), v("sy", s, s + 128)
 
-    for t in range(R):
-        ub = (v("qu2", 0, 128), v("su2", 0, 128))
+    ub = (v("qu2", 0, 128), v("su2", 0, 128))
+
+    def minus(b):
+        return v("ln", C * b, C * b + C, 2)
+
+    def own(a, src):
+        tt(v("m1", a, a + K), src, v("cmin", a, a + K), A.min)
+        scan(v("hh", a, a + K), v("khold", a, a + K), v("m1", a, a + K), -BIG, A.min, A.max)
+
+    def front():
+        quant(v("qx", K, C), v("sx", K, C), v("xt", 4 * K, 4 * C))
+        mm(bank(4, K), ub[0], ub[1], v("qx", K, C), v("sx", K, C))
+        own(K, bank(4, K))
+        quant(v("qx", 0, K), v("sx", 0, K), v("xt", 0, 4 * K))
         mm(bank(0, C), ub[0], ub[1], v("qx"), v("sx"))
-        mm(bank(2, C), v("qu2", 128, 256), v("su2", 128, 256), v("qx"), v("sx"))
+
+    front()
+    for t in range(R):
         mm(bank(1, C), ub[0], ub[1], v("qx"), v("sx"))
-        for a, b in ((K, C), (0, K)):
-            tt(v("m1", a, b), bank(0, b, a), v("cmin", a, b), A.min)
-            scan(v("hh", a, b), v("khold", a, b), v("m1", a, b), -BIG, A.min, A.max)
+        mm(bank(2, C), v("qu2", 128, 256), v("su2", 128, 256), v("qx"), v("sx"))
+        own(0, bank(0, K))
         act(v("sgb"), bank(2, C), F.Sign, bias=tiny_, scale=bit_)
         scan(v("bw"), v("stair"), v("sgb"), 0.0, A.max, A.mult)
-        act(v("x1"), ind(v("bw"), v("lu")), F.Identity, bias=is2_, scale=not2_)
+        act(v("x1"), ind(v("bw"), v("lu")), F.Identity, bias=is6_, scale=not6_)
         tt(v("pay"), ind(v("bw"), v("mu")), v("x1"), A.subtract)
         tt(slot(0), bank(0, C), v("hh"), A.is_le)
         scan(v("rd"), v("keep"), slot(0), 0.0, A.min, A.add)
-        tt(v("cxr", 15, C, 16), v("base"), v("rd", 15, C, 16), A.subtract)
+        tt(v("base2"), v("base"), v("rd", 15, C, 16), A.subtract)
         for c in range(23, 0, -1):
             z = c1("hh", 16 * c + 15)
-            if c > 2 * NPAIR:
-                s = v("sg", ROFF[c], ROFF[c + 1])
+            s, alone = v("sg", ROFF[c], ROFF[c + 1]), c1("rs", c) if c > 2 * NPAIR or c <= 2 * PAIR0 else None
+            if c in S_ROWS:
                 act(s, bank(1, 16 * c), F.Sign, bias=z, scale=-1.0)
-                act(slot(c), s, F.Relu, acc=c1("rs", c))
+                act(slot(c), s, F.Relu, acc=alone)
             else:
                 ts(slot(c), bank(0, 16 * c), z, A.is_lt)
-        for i in (2, 3, 4, 5, 1, 0):
+                if alone:
+                    act(s, slot(c), F.Identity, acc=alone)
+        for i in TORDER:
             a, w = TOFF[i], TILES[i]
-            if i != 5:
-                wq = 256 if i == 4 else w
-                quant(v("qc", a, a + wq), v("sc", a, a + wq), v("ct", 4 * a, 4 * (a + wq)))
+            quant(v("qc", a, a + w), v("sc", a, a + w), v("ct", 4 * a, 4 * (a + w)))
             if i == 2:
                 w = C
-            mm(bank(3, w), kq(0)[0], kq(0)[1], v("qc", a, a + w), v("sc", a, a + w), i == 2, i == 0)
+            mm(bank(3, w), kq(0)[0], kq(0)[1], v("qc", a, a + w), v("sc", a, a + w), i == 2, i == TORDER[-1])
             for bk, (ti, hf, a0, nw, calls, outs) in zip(SUMBANK, SUMS):
-                if ti == i and outs[0][0] < NPAIR:
+                if ti == i and PAIR0 <= outs[0][0] < NPAIR:
                     for j in range(calls):
                         x = a + a0 + nw * j
                         mm(bank(bk, nw), v("qr", 128 * hf, 128 * hf + 128), v("sr", 128 * hf, 128 * hf + 128),
                            v("qc", x, x + nw), v("sc", x, x + nw), j == 0, j == calls - 1)
                     for pr, x, nc in outs:
-                        act(v("jk", 160 * pr, 160 * pr + nc), bank(bk, x + nc, x), F.Identity, bias=-max(1.0, 128.0 / nc), acc=c1("pp", pr))
+                        act(v("jk", 160 * pr, 160 * pr + nc), bank(bk, x + nc, x), F.Identity, bias=-max(1.0, 128.0 / nc), acc=c1("rs", 2 * pr + 2))
         for b in range(4):
             mm(bank(4 + b, C), eq_(b)[0], eq_(b)[1], v("qx"), v("sx"))
             act(v("tv", 576 * b + K, 576 * b + 576), bank(4 + b, C), F.Copy)
-        odd, even = v("cxr", 31, 32 * NPAIR, 32), v("cxr", 47, 32 * NPAIR + 16, 32)
-        rest = v("cxr", 32 * NPAIR + 31, C, 16)
-        ts(v("ph", 0, NPAIR), v("pp", 0, NPAIR), ROUND, A.add, ROUND, A.subtract)
-        act(v("ph2", 0, NPAIR), v("pp", 0, NPAIR), F.Identity, bias=ROUND / 512, scale=1.0 / 512)
-        tt(even, even, v("pp", 0, NPAIR), A.subtract)
-        tt(even, even, v("ph", 0, NPAIR), A.add)
-        tt(odd, odd, v("ph2", 0, NPAIR), A.subtract)
-        tt(rest, rest, v("rs", 2 * NPAIR + 1, 24), A.subtract)
+        both = v("rs", 2 * PAIR0 + 2, 2 * NPAIR + 1, 2)
+        ts(v("ph", 2 * PAIR0 + 2, 2 * NPAIR + 1, 2), both, ROUND, A.add, ROUND, A.subtract)
+        aff(v("ph", 2 * PAIR0 + 1, 2 * NPAIR, 2), both, -1.0 / 512, -ROUND / 512)
+        tt(v("base2"), v("base2"), v("rs"), A.subtract)
+        tt(v("base2"), v("base2"), v("ph"), A.add)
         scan(v("xs"), bank(3, C), v("cxr"), -1.0, A.max, A.add)
-        ts(v("rk"), v("xs", 15, C, 16), 3072.0, A.add)
-        aff(v("cxr", 15, C, 16), v("base"), 0.0, end_)
+        tt(v("rk"), v("xs", 15, C, 16), v("base2"), A.add)
         cp(ind(v("pw"), v("rk")), v("pay"))
         turn(v("yt", 0, 192), v("pw", 0, 192))
         turn(v("yt", 192, 384), v("pw", 16, 208))
@@ -407,13 +417,19 @@ def build(T, topo, core):
         tt(v("fe"), v("fl"), v("ee"), A.mult)
         tt(v("lr", 0, 12), v("ab2", 0, 12), v("fe"), A.add)
         tt(v("lr", 12, 24), v("ab2", 12, 24), v("fe"), A.subtract)
-        cp(v("lru"), v("lr"))
-        act(v("ff"), ind(v("lr", 0, 12), v("repu")), F.Copy)
-        act(v("camp", 31, C, 32), v("lr", 0, 12), F.Identity, bias=-3.0, scale=-1.0 / 512)
-        for b in range(4):
+        tt(v("lru", 0, 12), v("ab2", 0, 12), v("fe"), A.add)
+        tt(v("lru", 12, 24), v("ab2", 12, 24), v("fe"), A.subtract)
+        cp(v("ff"), ind(v("lr", 0, 12), v("repu")))
+        ts(v("camp", 31, C, 32), v("lr", 0, 12), -1.0 / 512, A.mult, -3.0, A.add)
+        for b in (2, 0, 3, 1):
             tw = v("tv", 576 * b + K, 576 * b + 576)
-            act(v("ln", K * b, K * b + K), ind(tw, v("lru", 0, 12)), F.Copy)
-            tt(v("mt", b, 4 * K, 4), ind(tw, v("lru", 12, 24)), v("ln", K * b, K * b + K), A.subtract)
+            if b < 2 or not BY_SCAN:
+                act(minus(b), ind(tw, v("lru", 0, 12)), F.Identity, scale=-1.0)
+                tt(v("mt", b, 4 * K, 4), ind(tw, v("lru", 12, 24)), minus(b), A.add)
+            else:
+                act(minus(b), ind(tw, v("lru", 0, 12)), F.Identity, scale=-1.0)
+                act(v("ln", C * b + 1, C * b + C, 2), ind(tw, v("lru", 12, 24)), F.Copy)
+                scan(v("mt", b - 2, 4 * K, 2), v("two", 0, 2 * C, 2), v("ln", C * b, C * b + C), 0.0, A.mult, A.add)
         quant(v("qm"), v("smm"), v("mt"))
         arrived(t)
         for b in range(4):
@@ -425,7 +441,7 @@ def build(T, topo, core):
         quant(v("qh"), v("sh"), v("ht"))
         for b in range(4):
             mm(bank(b, K), eq_(b)[0], eq_(b)[1], v("qh"), v("sh"))
-            tt(v("tv", 576 * b, 576 * b + K), bank(b, K), v("ln", K * b, K * b + K), A.add)
+            tt(v("tv", 576 * b, 576 * b + K), bank(b, K), minus(b), A.subtract)
         tt(v("eq", 1, C, 2), ind(v("iot"), v("lru", 0, 12)), v("ff"), A.is_equal)
         tt(v("eq", K, C, 2), ind(v("iot"), v("lru", 0, 6)), v("ff", 96, K), A.is_equal)
         scan(v("es"), v("eq"), v("camp"), 0.0, A.max, A.add)
@@ -435,14 +451,15 @@ def build(T, topo, core):
             cp(ind(v("wh", 512 * t, 512 * t + 896), v("du", 2 * c, 2 * c + 2)), v("kv", 32 * c, 32 * c + 32))
         scan(v("xw"), v("wh", 512 * t + 512, 512 * t + 896), v("cxr"), -1.0, A.max, A.add)
         ts(v("wu"), v("xw", 15, C, 16), 3072.0, A.add)
-        for b in range(4):
-            w, x = v("tv", 576 * b, 576 * b + 576), XT_S[b]
-            if x:
-                act(v("xt", b, 64 * x, 4), ind(w, v("wu", 0, x)), F.Identity, scale=-2.0)
-            if x < 24:
-                ts(v("xt", 64 * x + b, 4 * C, 4), ind(w, v("wu", x, 24)), -2.0, A.mult)
+        for a in (12, 0):
+            for b in range(4):
+                w, x = v("tv", 576 * b, 576 * b + 576), a + XT_V.get((a, b), 0)
+                if x > a:
+                    ts(v("xt", 64 * a + b, 64 * x, 4), ind(w, v("wu", a, x)), -2.0, A.mult)
+                if x < a + 12:
+                    act(v("xt", 64 * x + b, 64 * a + 4 * K, 4), ind(w, v("wu", x, a + 12)), F.Identity, scale=-2.0)
         if t < R - 1:
-            quant(v("qx"), v("sx"), v("xt"))
+            front()
 
     cp(v("olu", 0, 12, 2), v("lr", 0, 6))
     cp(v("olu", 1, 12, 2), v("lr", 6, 12))
@@ -455,8 +472,8 @@ def build(T, topo, core):
         quant(v("qx", a, b), v("sx", a, b), v("xt", 4 * a, 4 * b))
         mm(bank(j, K), v("qv"), v("sv"), v("qx", a, b), v("sx", a, b))
         dma("y", lambda a=a, b=b: T.oc[:, 4 * a:4 * b], lambda a=a, b=b: T.qx[:, a:b].bitcast(dt.uint8), [v("qx", a, b)], [], 2700)
-    act(v("yf", 0, K), bank(0, K), F.Copy)
-    cp(v("yf", K, C), bank(1, K))
+    cp(v("yf", 0, K), bank(0, K))
+    act(v("yf", K, C), bank(1, K), F.Copy)
     dma("s", lambda: T.y[:, 0:K], lambda: T.yf[:, 0:K], [v("yf", 0, K)], [])
     dma("s", lambda: T.y[:, K:C], lambda: T.yf[:, K:C], [v("yf", K, C)], [])
     for k in range(4):
@@ -503,65 +520,88 @@ def plan(ops):
     tail = [0.0] * n
     for i in range(n - 1, -1, -1):
         tail[i] = ns[i] + max([0.0] + [lag[k][i] + tail[k] for k in after[i]])
-    pre = [[(j, ns[j] + lag[i][j]) for j in deps[i]] for i in range(n)]
+    behind = []
+    for i in range(n):
+        m = 0
+        for j in deps[i]:
+            if lag[i][j] >= 0:
+                m |= behind[j] | 1 << j
+        behind.append(m)
+    rng = np.random.RandomState(1)
 
-    def lay(key, lo, hi, busy, start):
-        busy, start = dict((q, list(b)) for q, b in busy.items()), list(start)
-        left = [0] * lo + [sum(1 for j in deps[i] if j >= lo) for i in range(lo, hi)] if (lo, hi) not in lefts else list(lefts[lo, hi])
-        lefts.setdefault((lo, hi), list(left))
-        ready = sorted((key[i], i) for i in range(lo, hi) if not left[i])
-        while ready:
-            i = ready.pop(0)[1]
-            s = 0.0
+    def vary(key, lo, hi, busy, start, passes):
+        m = hi - lo
+        soon = [max([0.0] + [start[j] + ns[j] + lag[i][j] for j in deps[i] if j < lo]) for i in range(lo, hi)]
+        pre = [[(j - lo, ns[j] + lag[i][j]) for j in deps[i] if j >= lo and
+                not any(lag[i][k] >= 0 and behind[k] >> j & 1 for k in deps[i])] for i in range(lo, hi)]
+        fed = [[] for _ in range(m)]
+        for i in range(m):
             for j, d in pre[i]:
-                if start[j] + d > s:
-                    s = start[j] + d
-            b, h = busy[qs[i]], hold[i]
-            k = len(b)
-            while k and b[k - 1][1] > s:
-                k -= 1
-            while k < len(b) and s + h > b[k][0]:
-                s = max(s, b[k][1])
-                k += 1
-            b.insert(k, (s, s + h))
-            start[i] = s
-            new = False
-            for k in after[i]:
-                if k < hi:
+                fed[j].append(i)
+        feeds = [[j for j, d in p] for p in pre]
+        t0 = min(soon)
+        q_of, h_of, mine = qs[lo:hi], hold[lo:hi], [i for i in range(m) if qs[lo + i] != "g"]
+        late = dict((q, [x for x in b if x[1] > t0]) for q, b in busy.items())
+
+        def lay(key):
+            now, at, left = dict((q, list(b)) for q, b in late.items()), list(soon), [len(p) for p in pre]
+            ready = sorted((key[i], i) for i in range(m) if not left[i])
+            while ready:
+                i = ready.pop(0)[1]
+                s = at[i]
+                for j, d in pre[i]:
+                    if at[j] + d > s:
+                        s = at[j] + d
+                b, h = now[q_of[i]], h_of[i]
+                k = len(b)
+                while k and b[k - 1][1] > s:
+                    k -= 1
+                while k < len(b) and s + h > b[k][0]:
+                    s = max(s, b[k][1])
+                    k += 1
+                b.insert(k, (s, s + h))
+                at[i] = s
+                new = False
+                for k in fed[i]:
                     left[k] -= 1
                     if not left[k]:
                         ready.append((key[k], k))
                         new = True
-            if new:
-                ready.sort()
-        return max(start[i] + ns[i] for i in range(lo, hi) if qs[i] != "g"), start, busy
+                if new:
+                    ready.sort()
+            last = max(at[i] + ns[lo + i] for i in mine)
+            return (at[-1] + 0.1 * last if q_of[-1] == "v" else last), at, now
 
-    lefts, rng = {}, np.random.RandomState(1)
-    cuts = [0] + [i + 1 for i in range(n) if ops[i][3][:1] == [v("qx")]] + [n]
-
-    def vary(key, lo, hi, busy, start, t0, passes):
-        best = now = lay(key, lo, hi, busy, start)
+        best = now = lay(key)
         for step in range(passes):
-            mid, wide = t0 + float(rng.rand()) * (now[0] - t0), 300 + 2500 * float(rng.rand())
-            at = np.array(now[1])
-            move = (np.abs(at - mid) < wide) & (rng.rand(n) < 0.15)
-            got = lay((at + move * rng.randn(n) * (200.0, 600.0, 2000.0)[step % 3]).tolist(), lo, hi, busy, start)
-            if got[0] <= now[0] + 100.0 * float(rng.rand()) * (1.0 - step / passes) ** 2:
+            at, far = np.array(now[1]), (200.0, 600.0, 2000.0)[step % 3]
+            if step % 2:
+                mid, wide = at[rng.randint(m)], 300 + 2500 * rng.rand()
+                at += ((np.abs(at - mid) < wide) & (rng.rand(m) < 0.1)) * rng.randn(m) * far
+            else:
+                kin, up = set([int(rng.randint(m))]), rng.rand() < 0.6
+                for _ in range(int(rng.randint(3))):
+                    kin |= set(j for i in kin for j in (feeds[i] if up else fed[i]))
+                at[list(kin)] += abs(rng.randn()) * far * (-1 if up else 1)
+            got = lay(at.tolist())
+            if got[0] <= now[0] + 100.0 * rng.rand() * (1.0 - step / passes) ** 2:
                 now = got
                 if now[0] < best[0]:
                     best = now
-        return best
+        start[lo:hi] = best[1]
+        busy.update(best[2])
 
-    busy, per = dict((q, []) for q in "vspgy"), cuts[2] - cuts[1]
-    one = vary([-x for x in tail], cuts[1], cuts[2], busy, [-1e5] * n, 0.0, 2 * PASSES)[1][cuts[1]:cuts[2]]
-    start, t0 = [0.0] * n, 0.0
+    cuts = [0] + [i + 1 for i in range(n) if ops[i][3] in ([bank(0, C)], [v("pw")])][1:] + [n]
+    busy, start, per = dict((q, []) for q in "vspgy"), [-1e5] * n, cuts[4] - cuts[2]
+    for lo, hi in zip(cuts[2:4], cuts[3:5]):
+        vary([-x for x in tail[lo:hi]], lo, hi, busy, start, 3 * PASSES)
+    one = start[cuts[2]:cuts[4]]
+    key = [1e9] * (cuts[2] - per) + [x + 4000.0 for x in one] + one + one + [1e9] * n
+    for i in range(cuts[2] - per - 1, -1, -1):
+        key[i] = min([1e9] + [key[k] - ns[i] - lag[k][i] for k in after[i] if k < cuts[2]])
+    busy, start = dict((q, []) for q in "vspgy"), [0.0] * n
     for lo, hi in zip(cuts, cuts[1:]):
-        a = hi - per if lo == 0 else lo
-        key = [1e9] * n
-        key[a:a + per] = [x + (t0 or 4000.0) for x in one]
-        for i in range(a - 1, lo - 1, -1):
-            key[i] = min([1e9] + [key[k] - ns[i] - lag[k][i] for k in after[i] if k < hi])
-        t0, start, busy = vary(key, lo, hi, busy, start, t0, 2 * PASSES if lo == 0 else PASSES // 2)
+        vary(key[lo:hi], lo, hi, busy, start, 3 * PASSES if lo == 0 else PASSES // 2)
     return sorted(range(n), key=lambda k: (start[k], k))
 
 

import numpy as np
from concourse.mybir import dt, AluOpType, AxisListType, ActivationFunctionType

A = AluOpType
F = ActivationFunctionType
C, K, R = 384, 192, 3
BIG = 2.0 ** 80
BF, F32, I32, U16, Q4, U8 = "bfloat16", "float32", "int32", "uint16", "float8_e4m3fn_x4", "uint8"
WIDE = {BF: 2, F32: 4, I32: 4, U16: 2, Q4: 4, U8: 1}
TILES = [384, 320, 256, 192, 128, 128]
SLOTS = [[0, 23, 22, 21], [20, 19, 18, 17], [16, 15, 14, 13], [12, 11, 10, 9], [8, 7, 6, 5], [4, 3, 2, 1]]
TOFF = [0, 384, 704, 1088, 1280, 1408]
NPAIR = 10
SUMS = [(2, 0, 0, 128, 2, [(7, 0, 128)]), (2, 1, 0, 128, 2, [(6, 0, 128)]), (3, 0, -64, 128, 2, [(5, 0, 128)]),
        (3, 1, -64, 128, 2, [(4, 0, 128)]), (4, 0, 0, 128, 1, [(3, 0, 128)]), (4, 1, 0, 128, 1, [(2, 0, 128)]),
        (1, 1, 0, 144, 2, [(8, 0, 144)]), (1, 0, 0, 160, 2, [(9, 0, 160)]), (5, 0, 0, 128, 1, [(1, 0, 64)]),
        (5, 1, 0, 128, 1, [(0, 0, 32)]), (0, 1, 0, 128, 3, [(10, 0, 128)])]
SUMBANK = [5, 6, 7, 4, 2, 5, 6, 7, 4, 2, 4]
PAIR0, S_ROWS, TORDER = 2, (23, 22, 21, 4, 3, 2, 1), (2, 3, 4, 1, 0, 5)
ROUND = 1.5 * 2.0 ** 32
XT_V = {(12, 2): 12, (12, 3): 12, (0, 3): 12, (0, 2): 4}
BY_SCAN = True
HT_V = (1, 3)
APART = 32768
TINY = 2.0 ** -110
ROFF = [8 * c * (c - 1) for c in range(25)]
CY, PE, GAT, SCA, WAKE = 0.85, 0.6, 1.5, 3.5, 180.0
PASSES = 12000


def _sb(n, d):
    return ("sbuf", [128, n], d)


SCRATCH = {
    "xt": _sb(4 * C, BF), "qx": _sb(C, Q4), "sx": _sb(C, U8),
    "ut": _sb(512, BF), "qu": _sb(128, Q4), "su": _sb(128, U8), "qu2": _sb(256, Q4), "su2": _sb(256, U8),
    "vt": _sb(512, BF), "qv": _sb(128, Q4), "sv": _sb(128, U8),
    "wq": _sb(512, Q4), "wp": _sb(512, U8),
    "wq0": _sb(512, Q4), "wp0": _sb(512, U8), "wq1": _sb(512, Q4), "wp1": _sb(512, U8), "wq2": _sb(512, Q4), "wp2": _sb(512, U8),
    "l32": _sb(24, I32), "m32": _sb(24, I32), "lu": _sb(24, U16), "mu": _sb(24, U16),
    "et": _sb(520, BF), "qe": _sb(512, Q4), "se": _sb(512, U8),
    "grp": _sb(512, BF), "byh": _sb(512, BF), "kt": _sb(1024, BF), "qk": _sb(256, Q4), "sk": _sb(256, U8),
    "kb": _sb(48, F32), "w1": _sb(48, F32), "b48": _sb(48, F32),
    "ct": _sb(4 * 1536, BF), "qc": _sb(1536, Q4), "sc": _sb(1536, U8),
    "jk": _sb(1760, F32), "sg": _sb(4416, BF), "two": _sb(2 * C, BF), "kr": _sb(516, BF), "qr": _sb(256, Q4), "sr": _sb(256, U8),
    "ph": _sb(24, F32),
    "cin": _sb(3 * 128, F32), "sm": _sb(5 * 128, F32),
    "p32": _sb(24, I32), "pu": _sb(24, U16), "c32": _sb(12, I32), "repu": _sb(12, U16),
    "pi": _sb(8, I32), "col": _sb(16, F32), "pk32": _sb(16, I32), "pkf": _sb(8, F32), "pku": _sb(16, U16),
    "cmin": _sb(C, F32), "khold": _sb(C, F32), "cxr": _sb(C, F32), "camp": _sb(C, F32), "keep": _sb(C, BF),
    "rw": _sb(96, F32), "base": _sb(24, F32), "base2": _sb(24, F32), "pk": _sb(24, F32), "pko": _sb(72, F32),
    "iot": _sb(C, F32), "stair": _sb(C, F32), "wh": _sb(2048, F32), "kv": _sb(K, F32),
    "m1": _sb(C, F32), "hh": _sb(C, F32), "rd": _sb(C, BF), "rs": _sb(24, F32), "xs": _sb(C, F32), "rk": _sb(24, U16),
    "sgb": _sb(C, BF), "bw": _sb(C, F32), "x1": _sb(C, F32), "pay": _sb(C, BF), "pw": _sb(416, BF),
    "yt": _sb(544, BF), "qy": _sb(136, Q4), "sy": _sb(136, U8),
    "ab2": _sb(24, F32), "ee": _sb(12, F32),
    "ppi": _sb(12, I32), "fl": _sb(12, I32), "fe": _sb(12, F32), "lr": _sb(24, F32), "lru": _sb(24, U16),
    "tv": _sb(4 * 576, BF), "ln": _sb(4 * C, BF), "mt": _sb(4 * K, BF), "qm": _sb(K, Q4), "smm": _sb(K, U8),
    "ht": _sb(4 * K, BF), "qh": _sb(K, Q4), "sh": _sb(K, U8),
    "ff": _sb(K, F32), "eq": _sb(C, F32), "es": _sb(C, F32), "du": _sb(12, U16),
    "xw": _sb(C, F32), "wu": _sb(24, U16), "olu": _sb(24, U16), "olf": _sb(C, F32), "yf": _sb(C, F32),
    "ps": ("psum", [128, 4096], F32),
}
NDMA = 24
SEMAPHORES = ["cv", "cs", "cp", "cg", "arr0", "arr1", "arr2", "sent"] + ["d%d" % i for i in range(NDMA)]
CSEM = {"v": "cv", "s": "cs", "p": "cp", "g": "cg"}


def v(name, a=0, b=None, s=1):
    if b is None:
        b = SCRATCH[name][1][1]
    return (name, a, b, s)


def bank(i, n, a=0, s=1):
    return ("ps", 512 * i + a, 512 * i + n, s)


def ind(win, off):
    return ("ind", win, off)


def _mask(w):
    if w[0] == "ps":
        return 1 << (w[1] // 512)
    m = 0
    if w[3] == 1:
        return ((1 << (w[2] - w[1])) - 1) << w[1]
    for i in range(w[1], w[2], w[3]):
        m |= 1 << i
    return m


def _n(w):
    return 16 * _n(w[2]) if w[0] == "ind" else len(range(w[1], w[2], w[3]))


def _vcost(o, i, base=None):
    if o[0] == "ind":
        return 50 + _n(i) * SCA * CY
    if i[0] == "ind":
        return 50 + _n(i) * max(GAT, base or 0) * CY
    if base is None:
        base = 0.5 if WIDE[SCRATCH[o[0]][2]] == 2 and WIDE[SCRATCH[i[0]][2]] == 2 else 1.0
    return max(64, _n(i) * base) * CY


def build(T, topo, core):
    ops = []

    def ap(w, cast=None):
        if not isinstance(w, tuple):
            return w
        if w[0] == "ind":
            return ap(w[1], cast).indirect(ap(w[2]))
        r = T[w[0]][:, w[1]:w[2]:w[3]] if w[3] != 1 else T[w[0]][:, w[1]:w[2]]
        return r.bitcast(cast) if cast is not None else r

    def flat(ws):
        r = []
        for w in ws:
            if isinstance(w, tuple):
                r += [w[1], w[2]] if w[0] == "ind" else [w]
        return r

    def add(q, fn, rd, wr, ns, kind="c"):
        rd, wr2 = flat(rd), []
        for w in wr:
            if w[0] == "ind":
                wr2.append(w[1])
                rd.append(w[2])
            else:
                wr2.append(w)
        ops.append((q, fn, rd, wr2, kind, ns))

    def ts(o, i, s1, op0, s2=None, op1=None):
        if op1 is None:
            add("v", lambda e: e.tensor_scalar(ap(o), ap(i), ap(s1), None, op0), [i, s1], [o], _vcost(o, i))
        else:
            add("v", lambda e: e.tensor_scalar(ap(o), ap(i), ap(s1), ap(s2), op0, op1), [i, s1, s2], [o], _vcost(o, i))

    def tt(o, a, b, op):
        add("v", lambda e: e.tensor_tensor(ap(o), ap(a), ap(b), op), [a, b], [o], _vcost(o, a, 1.0 if "ps" in (a[0], b[0]) else 2.0))

    def cp(o, i, cast=None):
        add("v", lambda e: e.tensor_copy(ap(o, cast), ap(i, cast)), [i], [o], _vcost(o, i))

    def ms(o, c):
        add("v", lambda e: e.memset(ap(o), c), [], [o], _vcost(o, o))

    def scan(o, a, b, init, op0, op1):
        add("v", lambda e: e.tensor_tensor_scan(ap(o), ap(a), ap(b), init, op0, op1), [a, b], [o], _vcost(o, a))

    def turn(o, i):
        add("v", lambda e: e.transpose(ap(o), ap(i)), [i], [o], _vcost(o, i))

    def quant(q, s, i):
        add("v", lambda e: e.quantize_mx(ap(q), ap(s), ap(i)), [i], [q, s], 12 + 0.265 * CY * _n(i))

    def act(o, i, f, bias=None, scale=None, acc=None):
        def fn(e):
            kw = {}
            if bias is not None:
                kw["bias"] = ap(bias)
            if scale is not None:
                kw["scale"] = ap(scale)
            if acc is not None:
                kw["accum_out"] = ap(acc)
            return e.activation(ap(o), ap(i), f, **kw)
        add("s", fn, [i, bias, scale], [o] + ([acc] if acc is not None else []),
            60 + (20 if acc is not None else 0) + _n(i) * CY * (GAT if i[0] == "ind" else 1))

    def mm(o, wq, ws, xq, xs, start=True, stop=True):
        add("p", lambda e: e.matmul_mx(ap(o), ap(wq), ap(ws), ap(xq), ap(xs), start, stop), [wq, ws, xq, xs], [o], (_n(xq) + 16) * PE)

    def iota(o, pat, base, cm):
        if SCRATCH[o[0]][2] == I32:
            add("g", lambda e: e.iota(ap(o), pat, base, cm), [], [o], 130 + 2 * CY * _n(o))
        else:
            add("g", lambda e: e.iota(ap(o), pat, base, cm, allow_small_or_imprecise_dtypes=True), [], [o], 130 + 2 * CY * _n(o))

    def sel(o, i, pat, op, fill, base, cm):
        add("g", lambda e: e.affine_select(ap(o), ap(i), pat, op, fill, base, cm), [i], [o], 170 + 2 * CY * _n(o))

    def dma(q, o, i, rd, wr, ns=2500):
        add(q, lambda e: e.dma_start(o(), i()), rd, wr, ns, "d")

    rank = T.rank_of(core)
    n = len(T.cores)
    dst, src = T.cores[(rank - 1) % n], T.cores[(rank + 1) % n]
    rid, pid, emask = topo.addr(dst)[0], topo.addr(dst)[1], topo.mask(core, dst)
    nout, nin = len(topo.engines(core, dst)), 2 * len(topo.engines(src, core))

    def send(t):
        q, s = ("wq%d" % (t - 1), "wp%d" % (t - 1)) if t else ("wq", "wp")
        if t:
            add("g", lambda e: e.wait_ge(T.sem["arr%d" % (t - 1)], nin), [v(q, 0, 1), v(s, 0, 1)], [], 1, "w")
        add("g", lambda e: e.remote_dma(ap(v("wq%d" % t), dt.uint8), ap(v(q), dt.uint8), T.sem["arr%d" % t], T.sem.sent, pid, rid, emask),
            [v(q, 0, 1)], [v("wq%d" % t, 0, 1)], 9000, ("r", nout))
        add("g", lambda e: e.remote_dma(ap(v("wp%d" % t)), ap(v(s)), T.sem["arr%d" % t], T.sem.sent, pid, rid, emask),
            [v(s, 0, 1)], [v("wp%d" % t, 0, 1)], 9000, ("r", nout))

    def arrived(t):
        add("p", lambda e: e.wait_ge(T.sem["arr%d" % t], nin), [v("qm")], [v("wq%d" % t, 2, 512), v("wp%d" % t, 2, 512)], 1, "w")

    def c1(name, j):
        return v(name, j, j + 1)

    dma("y", lambda: T.ut[:], lambda: T.u[:], [], [v("ut")])
    dma("s", lambda: T.xt[:, 768:1536], lambda: T.x[:, 768:1536], [], [v("xt", 768, 1536)], 3000)
    dma("y", lambda: T.xt[:, 0:768], lambda: T.x[:, 0:768], [], [v("xt", 0, 768)], 3000)
    dma("y", lambda: T.l32[:], lambda: T.l[:], [], [v("l32")])
    dma("y", lambda: T.m32[:], lambda: T.m[:], [], [v("m32")])
    dma("y", lambda: T.wq[:].bitcast(dt.uint8), lambda: T.wc[:], [], [v("wq")], 4000)
    dma("y", lambda: T.wp[:], lambda: T.ws[:], [], [v("wp")], 4000)
    dma("y", lambda: T.vt[:], lambda: T.v[:], [], [v("vt")])

    def aff(o, i, scale, bias):
        act(o, i, F.Identity, bias=bias, scale=scale)

    ms(v("cin", 0, 128), BIG)
    ms(v("two"), 0.0)
    quant(v("qc", 960, 1088), v("sc", 960, 1088), v("two", 0, 512))
    aff(v("two", 2, 2 * C, 4), v("two", 2, 2 * C, 4), 1.0, 1.0)
    aff(v("two", 3, 516, 4), v("two", 3, 516, 4), 1.0, 512.0)
    iota(v("p32"), [[0, 24]], 0, 1)
    sel(v("sm", 0, 128), v("cin", 0, 128), [[1, 128]], A.is_equal, -BIG, 0, -1)
    sel(v("sm", 128, 256), v("cin", 0, 128), [[1, 128]], A.is_gt, -BIG, 0, -1)
    iota(v("pk32"), [[0, 2], [16, 8]], 0, 0)
    iota(v("grp"), [[1, 8], [0, 64]], 0, 0)
    sel(v("kr"), v("two", 0, 516), [[-1, 129], [0, 4]], A.is_equal, 0.0, 0, 1)
    aff(v("two", 1, 520, 4), v("two", 1, 520, 4), 1.0, -0.5)
    iota(v("iot"), [[1, C]], 0, 0)
    iota(v("cin", 128, 384), [[-1022, 2], [0, 128]], 1024, 0)
    sel(v("sm", 256, 384), v("cin", 128, 256), [[1, 128]], A.is_equal, 0.0, 0, -1)
    iota(v("base"), [[16, 24]], 3072 + 15, 0)
    sel(v("sm", 384, 512), v("sm", 256, 384), [[1, 128]], A.is_ge, -4096.0, 0, -1)
    ms(v("keep"), 64.0)
    ms(v("keep", 0, C, 16), 0.0)
    sel(v("et"), v("two", 0, 520), [[-1, 520]], A.is_equal, 0.0, 5, 4)
    send(0)
    iota(v("byh"), [[0, 4], [APART - 1, 2], [0, 64]], 1, 0)
    sel(v("kt", 512, 1024), v("byh"), [[0, 8], [-1, 16], [0, 4]], A.is_equal, 0.0, 0, 1)
    sel(v("sm", 512, 640), v("cin", 256, 384), [[1, 128]], A.is_ge, 0.0, 0, -1)
    iota(v("c32"), [[1, 12]], 0, 0)
    iota(v("kv"), [[16, 6], [96, 2], [1, 16]], 0, 0)
    iota(v("wh", 0, 1024), [[0, 2], [1, 512]], K, 0)
    send(1)
    iota(v("wh", 1024, 2048), [[0, 2], [1, 512]], K, 0)
    send(2)

    cp(v("pu"), v("p32"))
    ts(c1("pi", 0), c1("p32", 0), 1, A.bitwise_and)
    ts(c1("pi", 1), c1("p32", 0), 2, A.logical_shift_right, 2, A.bitwise_and)
    ts(c1("pi", 2), c1("p32", 0), 15, A.bitwise_and)
    ts(c1("pi", 3), c1("p32", 0), 4, A.logical_shift_right, 1, A.bitwise_and)
    ts(c1("pi", 4), c1("p32", 0), 4, A.logical_shift_right)
    cp(v("col", 0, 5), v("pi", 0, 5))
    q_, h_, g_, bit_, tiny_, not6_, is6_, hq_, nh_, junk_, junk2_, s1_, s2_ = [c1("col", j) for j in range(2, 15)]
    cp(v("pku", 0, 8), v("pk32", 0, 8))
    ts(v("pkf"), v("pk32", 8, 16), c1("col", 0), A.add, c1("col", 1), A.add)
    ts(v("pku", 8, 16), v("pkf"), 1.0, A.add)
    act(v("cmin"), ind(v("sm", 0, 128), v("pu")), F.Copy)
    act(v("khold"), ind(v("sm", 128, 256), v("pu")), F.Copy)
    for i in range(6):
        ms(v("ct", 4 * (TOFF[i] + 16 * SLOTS[i][3]), 4 * (TOFF[i] + TILES[i])), 0.0)
    for j in range(2):
        quant(v("qr", 128 * j, 128 * j + 128), v("sr", 128 * j, 128 * j + 128), v("kr", 2 - 2 * j, 514 - 2 * j))
    ms(v("rs"), 0.0)
    aff(v("ph"), v("rs"), 1.0, 0.0)
    ms(v("pw", 0, 16), 0.0)
    ms(v("yt", 384, 544), 0.0)
    ms(v("rw", 0, 32), 0.0)
    for a, b, w in ((0, 13, 0.5), (1, 12, 8.0), (8, 5, 128.0), (9, 4, 2048.0)):
        aff(v("rw", a, a + 17, 16), v("rw", a, a + 17, 16), 1.0, w)
        aff(v("rw", b, b + 17, 16), v("rw", b, b + 17, 16), 1.0, w / 4096 / APART)
    aff(v("rw", 6, 15, 8), v("rw", 6, 15, 8), 1.0, 1024.0)
    aff(v("rw", 7, 31, 23), v("rw", 7, 31, 23), 1.0, float(K))
    quant(v("qu"), v("su"), v("ut"))
    for j in range(2):
        cp(v("qu2", 128 * j, 128 * j + 128), ind(v("qu"), v("pku", 8 * j, 8 * j + 8)), dt.uint32)
        act(v("su2", 128 * j, 128 * j + 128), ind(v("su"), v("pku", 8 * j, 8 * j + 8)), F.Copy)
    tt(v("rw", 32, 64), v("rw", 0, 32), v("cmin", 0, 32), A.min)
    scan(v("rw", 64, 96), v("khold", 0, 32), v("rw", 32, 64), -BIG, A.min, A.max)
    top_, foot_ = c1("rw", 79), c1("rw", 95)
    ts(v("stair"), v("iot"), top_, A.min, foot_, A.max)
    tt(bit_, top_, foot_, A.is_equal)
    ts(tiny_, bit_, 0.0, A.is_equal, -TINY, A.add)
    ts(v("kt", 0, 512), v("grp"), g_, A.is_equal)
    quant(v("qk", 0, 128), v("sk", 0, 128), v("kt", 0, 512))
    cp(v("lu"), v("l32"))
    cp(v("mu"), v("m32"))
    ts(not6_, q_, 6.0, A.not_equal)
    aff(is6_, not6_, -float(K), float(K))
    act(v("cxr"), ind(v("sm", 384, 512), v("pu")), F.Copy)
    aff(v("cxr", 15, C, 16), v("cxr", 15, C, 16), 1.0, -4096.0)
    ts(hq_, h_, 16.0, A.mult, q_, A.subtract)
    aff(v("base"), v("base"), 1.0, hq_)
    aff(v("base", 2 * PAIR0 + 1, 2 * NPAIR, 2), v("base", 2 * PAIR0 + 1, 2 * NPAIR, 2), 1.0, ROUND / 512)
    aff(v("base", 2 * PAIR0 + 2, 2 * NPAIR + 1, 2), v("base", 2 * PAIR0 + 2, 2 * NPAIR + 1, 2), 1.0, -128.0)
    for c in (18, 20):
        aff(c1("base", c), c1("base", c), 1.0, 128.0 - 8.0 * c)
    aff(nh_, h_, -float(APART), float(APART))
    aff(junk_, q_, 1.0, 384.0)
    aff(junk2_, q_, 1.0, 400.0)
    quant(v("qk", 128, 256), v("sk", 128, 256), v("kt", 512, 1024))
    ms(v("kb"), 1.0)
    aff(v("kb", 0, 48, 4), v("kb", 0, 48, 4), 0.0, 0.0)
    aff(v("kb", 2, 48, 4), v("kb", 2, 48, 4), nh_, 0.0)
    aff(s1_, h_, -2048.0, 1024.0)
    aff(s2_, h_, 1024.0, -1536.0)
    aff(v("pk", 0, 24, 2), v("kb", 1, 48, 4), s1_, 0.0)
    aff(v("pk", 1, 24, 2), v("kb", 1, 48, 4), s2_, 0.0)
    for b in range(4):
        quant(v("qe", 128 * b, 128 * b + 128), v("se", 128 * b, 128 * b + 128), v("et", 5 - b, 517 - b))
    ms(v("eq", 0, K, 2), 0.0)
    act(v("camp", 0, C, 2), ind(v("sm", 512, 640), v("pu", 0, 12)), F.Copy)
    act(v("camp", 1, C, 2), ind(v("sm", 512, 640), v("pu", 0, 12)), F.Identity, scale=-1.0)
    cp(v("repu"), v("c32"))
    quant(v("qv"), v("sv"), v("vt"))

    def slot(c):
        for i in range(6):
            if c in SLOTS[i]:
                w = 16 * c if c else C
                a = 4 * TOFF[i] + SLOTS[i].index(c)
                return v("ct", a, a + 4 * w - 3, 4)

    def kq(i):
        return v("qk", 128 * i, 128 * i + 128), v("sk", 128 * i, 128 * i + 128)

    def eq_(b):
        return v("qe", 128 * b, 128 * b + 128), v("se", 128 * b, 128 * b + 128)

    def ym(s):
        return v("qy", s, s + 128), v("sy", s, s + 128)

    ub = (v("qu2", 0, 128), v("su2", 0, 128))

    def minus(b):
        return v("ln", C * b, C * b + C, 2)

    def own(a, src):
        tt(v("m1", a, a + K), src, v("cmin", a, a + K), A.min)
        scan(v("hh", a, a + K), v("khold", a, a + K), v("m1", a, a + K), -BIG, A.min, A.max)

    def front():
        quant(v("qx", K, C), v("sx", K, C), v("xt", 4 * K, 4 * C))
        mm(bank(4, K), ub[0], ub[1], v("qx", K, C), v("sx", K, C))
        own(K, bank(4, K))
        quant(v("qx", 0, K), v("sx", 0, K), v("xt", 0, 4 * K))
        mm(bank(0, C), ub[0], ub[1], v("qx"), v("sx"))

    front()
    for t in range(R):
        mm(bank(1, C), ub[0], ub[1], v("qx"), v("sx"))
        mm(bank(2, C), v("qu2", 128, 256), v("su2", 128, 256), v("qx"), v("sx"))
        own(0, bank(0, K))
        act(v("sgb"), bank(2, C), F.Sign, bias=tiny_, scale=bit_)
        scan(v("bw"), v("stair"), v("sgb"), 0.0, A.max, A.mult)
        act(v("x1"), ind(v("bw"), v("lu")), F.Identity, bias=is6_, scale=not6_)
        tt(v("pay"), ind(v("bw"), v("mu")), v("x1"), A.subtract)
        tt(slot(0), bank(0, C), v("hh"), A.is_le)
        scan(v("rd"), v("keep"), slot(0), 0.0, A.min, A.add)
        tt(v("base2"), v("base"), v("rd", 15, C, 16), A.subtract)
        for c in range(23, 0, -1):
            z = c1("hh", 16 * c + 15)
            s, alone = v("sg", ROFF[c], ROFF[c + 1]), c1("rs", c) if c > 2 * NPAIR or c <= 2 * PAIR0 else None
            if c in S_ROWS:
                act(s, bank(1, 16 * c), F.Sign, bias=z, scale=-1.0)
                act(slot(c), s, F.Relu, acc=alone)
            else:
                ts(slot(c), bank(0, 16 * c), z, A.is_lt)
                if alone:
                    act(s, slot(c), F.Identity, acc=alone)
        for i in TORDER:
            a, w = TOFF[i], TILES[i]
            quant(v("qc", a, a + w), v("sc", a, a + w), v("ct", 4 * a, 4 * (a + w)))
            if i == 2:
                w = C
            mm(bank(3, w), kq(0)[0], kq(0)[1], v("qc", a, a + w), v("sc", a, a + w), i == 2, i == TORDER[-1])
            for bk, (ti, hf, a0, nw, calls, outs) in zip(SUMBANK, SUMS):
                if ti == i and PAIR0 <= outs[0][0] < NPAIR:
                    for j in range(calls):
                        x = a + a0 + nw * j
                        mm(bank(bk, nw), v("qr", 128 * hf, 128 * hf + 128), v("sr", 128 * hf, 128 * hf + 128),
                           v("qc", x, x + nw), v("sc", x, x + nw), j == 0, j == calls - 1)
                    for pr, x, nc in outs:
                        act(v("jk", 160 * pr, 160 * pr + nc), bank(bk, x + nc, x), F.Identity, bias=-max(1.0, 128.0 / nc), acc=c1("rs", 2 * pr + 2))
        for b in range(4):
            mm(bank(4 + b, C), eq_(b)[0], eq_(b)[1], v("qx"), v("sx"))
            act(v("tv", 576 * b + K, 576 * b + 576), bank(4 + b, C), F.Copy)
        both = v("rs", 2 * PAIR0 + 2, 2 * NPAIR + 1, 2)
        ts(v("ph", 2 * PAIR0 + 2, 2 * NPAIR + 1, 2), both, ROUND, A.add, ROUND, A.subtract)
        aff(v("ph", 2 * PAIR0 + 1, 2 * NPAIR, 2), both, -1.0 / 512, -ROUND / 512)
        tt(v("base2"), v("base2"), v("rs"), A.subtract)
        tt(v("base2"), v("base2"), v("ph"), A.add)
        scan(v("xs"), bank(3, C), v("cxr"), -1.0, A.max, A.add)
        tt(v("rk"), v("xs", 15, C, 16), v("base2"), A.add)
        cp(ind(v("pw"), v("rk")), v("pay"))
        turn(v("yt", 0, 192), v("pw", 0, 192))
        turn(v("yt", 192, 384), v("pw", 16, 208))
        quant(v("qy"), v("sy"), v("yt"))
        tt(v("w1"), v("yt", 4, 384, 8), v("yt", 5, 384, 8), A.add)
        scan(v("b48"), v("kb"), v("w1"), 0.0, A.mult, A.add)
        for j in range(2):
            mm(bank(0, 128), kq(1)[0], kq(1)[1], ym(2 * j)[0], ym(2 * j)[1], j == 0, j == 1)
        scan(v("pko", 0, 24), v("yt", 6, 384, 16), v("pk"), -512.0, A.max, A.add)
        scan(v("pko", 24, 48), v("yt", 7, 384, 16), v("pk"), -512.0, A.max, A.add)
        scan(v("pko", 48, 72), v("yt", 14, 384, 16), v("pk"), 512.0, A.min, A.subtract)
        ts(v("ab2", 12, 24), v("pko", 1, 24, 2), 512.0 + K, A.add)
        tt(v("ee"), v("pko", 25, 48, 2), v("pko", 49, 72, 2), A.add)
        tt(v("ab2", 0, 12), v("ab2", 12, 24), v("ee"), A.subtract)
        tt(v("ppi"), bank(0, 96, 0, 8), v("b48", 3, 48, 4), A.mult)
        ts(v("fl"), v("ppi"), 3, A.arith_shift_right, 1, A.bitwise_and)
        tt(v("fe"), v("fl"), v("ee"), A.mult)
        tt(v("lr", 0, 12), v("ab2", 0, 12), v("fe"), A.add)
        tt(v("lr", 12, 24), v("ab2", 12, 24), v("fe"), A.subtract)
        tt(v("lru", 0, 12), v("ab2", 0, 12), v("fe"), A.add)
        tt(v("lru", 12, 24), v("ab2", 12, 24), v("fe"), A.subtract)
        cp(v("ff"), ind(v("lr", 0, 12), v("repu")))
        ts(v("camp", 31, C, 32), v("lr", 0, 12), -1.0 / 512, A.mult, -3.0, A.add)
        for b in (2, 0, 3, 1):
            tw = v("tv", 576 * b + K, 576 * b + 576)
            if b < 2 or not BY_SCAN:
                act(minus(b), ind(tw, v("lru", 0, 12)), F.Identity, scale=-1.0)
                tt(v("mt", b, 4 * K, 4), ind(tw, v("lru", 12, 24)), minus(b), A.add)
            else:
                act(minus(b), ind(tw, v("lru", 0, 12)), F.Identity, scale=-1.0)
                act(v("ln", C * b + 1, C * b + C, 2), ind(tw, v("lru", 12, 24)), F.Copy)
                scan(v("mt", b - 2, 4 * K, 2), v("two", 0, 2 * C, 2), v("ln", C * b, C * b + C), 0.0, A.mult, A.add)
        quant(v("qm"), v("smm"), v("mt"))
        arrived(t)
        for b in range(4):
            mm(bank(4 + b, K), v("wq%d" % t, 128 * b, 128 * b + 128), v("wp%d" % t, 128 * b, 128 * b + 128), v("qm"), v("smm"))
            if b in HT_V:
                ts(v("ht", b, 4 * K, 4), bank(4 + b, K), 0.03125, A.mult)
            else:
                act(v("ht", b, 4 * K, 4), bank(4 + b, K), F.Identity, scale=0.03125)
        quant(v("qh"), v("sh"), v("ht"))
        for b in range(4):
            mm(bank(b, K), eq_(b)[0], eq_(b)[1], v("qh"), v("sh"))
            tt(v("tv", 576 * b, 576 * b + K), bank(b, K), minus(b), A.subtract)
        tt(v("eq", 1, C, 2), ind(v("iot"), v("lru", 0, 12)), v("ff"), A.is_equal)
        tt(v("eq", K, C, 2), ind(v("iot"), v("lru", 0, 6)), v("ff", 96, K), A.is_equal)
        scan(v("es"), v("eq"), v("camp"), 0.0, A.max, A.add)
        ts(v("du", 0, 12, 2), v("es", 31, K, 32), -512.0, A.mult, junk_, A.max)
        ts(v("du", 1, 12, 2), v("es", K + 31, C, 32), -512.0, A.mult, junk2_, A.max)
        for c in range(5, -1, -1):
            cp(ind(v("wh", 512 * t, 512 * t + 896), v("du", 2 * c, 2 * c + 2)), v("kv", 32 * c, 32 * c + 32))
        scan(v("xw"), v("wh", 512 * t + 512, 512 * t + 896), v("cxr"), -1.0, A.max, A.add)
        ts(v("wu"), v("xw", 15, C, 16), 3072.0, A.add)
        for a in (12, 0):
            for b in range(4):
                w, x = v("tv", 576 * b, 576 * b + 576), a + XT_V.get((a, b), 0)
                if x > a:
                    ts(v("xt", 64 * a + b, 64 * x, 4), ind(w, v("wu", a, x)), -2.0, A.mult)
                if x < a + 12:
                    act(v("xt", 64 * x + b, 64 * a + 4 * K, 4), ind(w, v("wu", x, a + 12)), F.Identity, scale=-2.0)
        if t < R - 1:
            front()

    cp(v("olu", 0, 12, 2), v("lr", 0, 6))
    cp(v("olu", 1, 12, 2), v("lr", 6, 12))
    cp(v("olu", 12, 24, 2), v("lr", 12, 18))
    cp(v("olu", 13, 24, 2), v("lr", 18, 24))
    act(v("olf"), ind(v("iot"), v("olu")), F.Copy)
    dma("y", lambda: T.ol[:], lambda: T.olf[0:128:16, :], [v("olf")], [])
    for j in range(2):
        a, b = K * j, K * j + K
        quant(v("qx", a, b), v("sx", a, b), v("xt", 4 * a, 4 * b))
        mm(bank(j, K), v("qv"), v("sv"), v("qx", a, b), v("sx", a, b))
        dma("y", lambda a=a, b=b: T.oc[:, 4 * a:4 * b], lambda a=a, b=b: T.qx[:, a:b].bitcast(dt.uint8), [v("qx", a, b)], [], 2700)
    cp(v("yf", 0, K), bank(0, K))
    act(v("yf", K, C), bank(1, K), F.Copy)
    dma("s", lambda: T.y[:, 0:K], lambda: T.yf[:, 0:K], [v("yf", 0, K)], [])
    dma("s", lambda: T.y[:, K:C], lambda: T.yf[:, K:C], [v("yf", K, C)], [])
    for k in range(4):
        dma("y", lambda k=k: T.osc[4 * k:4 * k + 4, :], lambda k=k: T.sx[32 * k:32 * k + 4, :], [v("sx")], [])
    return ops


def clashes(ops):
    hist, out = {}, []
    for i, o in enumerate(ops):
        deps = {}
        for ws, w in ((o[2], False), (o[3], True)):
            for x in ws:
                m = _mask(x)
                for (j, mj, wj) in hist.get(x[0], []):
                    if m & mj and (w or wj or (x[0] == "ps" and ops[j][0] != o[0])):
                        deps[j] = True
        for ws, w in ((o[2], False), (o[3], True)):
            for x in ws:
                hist.setdefault(x[0], []).append((i, _mask(x), w))
        out.append(deps)
    return out


def inline(a, b):
    return a[0] == b[0] == "p"


def plan(ops):
    deps, n = clashes(ops), len(ops)
    after = [[] for o in ops]
    for i in range(n):
        for j in deps[i]:
            after[j].append(i)
    lag = [dict((j, 0.0 if inline(ops[j], ops[i]) else WAKE) for j in deps[i]) for i in range(n)]
    ns, qs = [o[5] for o in ops], [o[0] for o in ops]
    hold = [o[5] if o[4] in ("c", "w") else 60.0 if o[4] == "d" else 500.0 for o in ops]
    for chain in ([i for i in range(n) if qs[i] == "y" and not ops[i][2]], [i for i in range(n) if qs[i] == "g"]):
        for j, i in zip(chain, chain[1:]):
            if j not in deps[i]:
                deps[i][j] = True
                lag[i][j] = hold[j] - ns[j]
                after[j].append(i)
    tail = [0.0] * n
    for i in range(n - 1, -1, -1):
        tail[i] = ns[i] + max([0.0] + [lag[k][i] + tail[k] for k in after[i]])
    behind = []
    for i in range(n):
        m = 0
        for j in deps[i]:
            if lag[i][j] >= 0:
                m |= behind[j] | 1 << j
        behind.append(m)
    rng = np.random.RandomState(1)

    def vary(key, lo, hi, busy, start, passes):
        m = hi - lo
        soon = [max([0.0] + [start[j] + ns[j] + lag[i][j] for j in deps[i] if j < lo]) for i in range(lo, hi)]
        pre = [[(j - lo, ns[j] + lag[i][j]) for j in deps[i] if j >= lo and
                not any(lag[i][k] >= 0 and behind[k] >> j & 1 for k in deps[i])] for i in range(lo, hi)]
        fed = [[] for _ in range(m)]
        for i in range(m):
            for j, d in pre[i]:
                fed[j].append(i)
        feeds = [[j for j, d in p] for p in pre]
        t0 = min(soon)
        q_of, h_of, mine = qs[lo:hi], hold[lo:hi], [i for i in range(m) if qs[lo + i] != "g"]
        late = dict((q, [x for x in b if x[1] > t0]) for q, b in busy.items())

        def lay(key):
            now, at, left = dict((q, list(b)) for q, b in late.items()), list(soon), [len(p) for p in pre]
            ready = sorted((key[i], i) for i in range(m) if not left[i])
            while ready:
                i = ready.pop(0)[1]
                s = at[i]
                for j, d in pre[i]:
                    if at[j] + d > s:
                        s = at[j] + d
                b, h = now[q_of[i]], h_of[i]
                k = len(b)
                while k and b[k - 1][1] > s:
                    k -= 1
                while k < len(b) and s + h > b[k][0]:
                    s = max(s, b[k][1])
                    k += 1
                b.insert(k, (s, s + h))
                at[i] = s
                new = False
                for k in fed[i]:
                    left[k] -= 1
                    if not left[k]:
                        ready.append((key[k], k))
                        new = True
                if new:
                    ready.sort()
            last = max(at[i] + ns[lo + i] for i in mine)
            return (at[-1] + 0.1 * last if q_of[-1] == "v" else last), at, now

        best = now = lay(key)
        for step in range(passes):
            at, far = np.array(now[1]), (200.0, 600.0, 2000.0)[step % 3]
            if step % 2:
                mid, wide = at[rng.randint(m)], 300 + 2500 * rng.rand()
                at += ((np.abs(at - mid) < wide) & (rng.rand(m) < 0.1)) * rng.randn(m) * far
            else:
                kin, up = set([int(rng.randint(m))]), rng.rand() < 0.6
                for _ in range(int(rng.randint(3))):
                    kin |= set(j for i in kin for j in (feeds[i] if up else fed[i]))
                at[list(kin)] += abs(rng.randn()) * far * (-1 if up else 1)
            got = lay(at.tolist())
            if got[0] <= now[0] + 100.0 * rng.rand() * (1.0 - step / passes) ** 2:
                now = got
                if now[0] < best[0]:
                    best = now
        start[lo:hi] = best[1]
        busy.update(best[2])

    cuts = [0] + [i + 1 for i in range(n) if ops[i][3] in ([bank(0, C)], [v("pw")])][1:] + [n]
    busy, start, per = dict((q, []) for q in "vspgy"), [-1e5] * n, cuts[4] - cuts[2]
    for lo, hi in zip(cuts[2:4], cuts[3:5]):
        vary([-x for x in tail[lo:hi]], lo, hi, busy, start, 3 * PASSES)
    one = start[cuts[2]:cuts[4]]
    key = [1e9] * (cuts[2] - per) + [x + 4000.0 for x in one] + one + one + [1e9] * n
    for i in range(cuts[2] - per - 1, -1, -1):
        key[i] = min([1e9] + [key[k] - ns[i] - lag[k][i] for k in after[i] if k < cuts[2]])
    busy, start = dict((q, []) for q in "vspgy"), [0.0] * n
    for lo, hi in zip(cuts, cuts[1:]):
        vary(key[lo:hi], lo, hi, busy, start, 3 * PASSES if lo == 0 else PASSES // 2)
    return sorted(range(n), key=lambda k: (start[k], k))


def order(ops):
    deps, waits, clock = clashes(ops), [], []
    known = dict((q, set()) for q in "vspgy")
    mine = dict((q, set()) for q in "vspgy")
    for i, o in enumerate(ops):
        need = []
        for j in sorted(deps[i], reverse=True):
            if j not in known[o[0]] and ops[j][4] in ("c", "d") and o[4] != "w" and not inline(ops[j], o):
                need.append(j)
                known[o[0]] |= clock[j]
        waits.append(need)
        if o[4] == "c":
            mine[o[0]].add(i)
            clock.append(known[o[0]] | mine[o[0]])
        else:
            clock.append(known[o[0]] | set([i]))
    return waits


LAID = []


def rank_program(g, core, T, topo):
    if T.rank_of(core) is None:
        return
    ops = build(T, topo, core)
    if not LAID:
        seq = plan(ops)
        LAID.extend([seq, order([ops[i] for i in seq])])
    ops, waits = [ops[i] for i in LAID[0]], LAID[1]
    eng = {"v": g.vector, "s": g.scalar, "p": g.tensor, "g": g, "y": g.sync}
    needed = set(j for w in waits for j in w)
    where, count, ndma, sent, open_dma = {}, dict((q, 0) for q in CSEM), 0, 0, []
    for i, (q, fn, rd, wr, kind, ns) in enumerate(ops):
        for j in waits[i]:
            eng[q].wait_ge(where[j][0], where[j][1])
        r = fn(eng[q])
        if kind == "d":
            where[i] = (T.sem["d%d" % ndma], 16)
            ndma += 1
            r.then_inc(where[i][0], 16)
            if i not in needed:
                open_dma.append(i)
        elif kind == "c" and i in needed:
            count[q] += 1
            where[i] = (T.sem[CSEM[q]], count[q])
            r.then_inc(where[i][0], 1)
        elif isinstance(kind, tuple):
            sent += kind[1]
    g.wait_ge(T.sem.sent, sent)
    for i in open_dma:
        g.sync.wait_ge(where[i][0], 16)
